import numpy as np
import ml_dtypes


def mxq(x, axis, fmt="e4m3"):
    dtype, down = {"e4m3": (ml_dtypes.float8_e4m3fn, 7), "e5m2": (ml_dtypes.float8_e5m2, 14)}[fmt]
    v = np.moveaxis(np.asarray(x, np.float32).astype(ml_dtypes.bfloat16).astype(np.float64), axis, -1)
    blocks = v.reshape(v.shape[:-1] + (-1, 32))
    amax = np.abs(blocks).max(-1, keepdims=True)
    byte = np.maximum(np.where(amax > 0, np.frexp(amax)[1] - 1 + 127, 0) - down, 1)
    scale = np.exp2(byte - 127.0)
    codes = (blocks / scale).astype(np.float32).astype(dtype).astype(np.float64)
    return np.moveaxis((codes * scale).reshape(v.shape), -1, axis)


WIDE = False


def mx_kscale(k):
    if not WIDE:
        return np.ones(k)
    levels = np.array([10, -10, 5, -5, 0])
    if k % 512:
        return np.exp2(np.random.permutation(np.resize(levels, k // 32))).repeat(32)
    a = np.empty((k // 512, 16))
    for p in range(k // 512):
        a[p, :8] = np.random.permutation(np.resize(levels, 8))
        for g in range(8):
            far = levels[np.abs(levels - a[p, g]) >= 10]
            a[p, g + 8] = far[np.random.randint(len(far))]
    return np.exp2(a.ravel()).repeat(32)


BF16 = ml_dtypes.bfloat16


def bf(x):
    return np.asarray(x, np.float32).astype(BF16)


def f64(x):
    return np.asarray(x).astype(np.float64)


E2M1 = np.array([0.0, 0.5, 1.0, 1.5, 2.0, 3.0, 4.0, 6.0, -0.0, -0.5, -1.0, -1.5, -2.0, -3.0, -4.0, -6.0])


def pack_weight(w, fmt):
    k, n = w.shape
    w = f64(bf(w)).reshape(k // 32, 32, n)
    amax = np.abs(w).max(1)
    if fmt == "e4m3":
        byte = np.frexp(amax)[1] - 1 + 127 - 7
    else:
        mant, ex = np.frexp(amax / 6.0)
        byte = np.where(mant > 0.5, ex, ex - 1) + 127
    byte = np.clip(np.where(amax > 0, byte, 1), 1, 254)
    scaled = (w * np.exp2(127.0 - byte)[:, None, :]).reshape(k, n).astype(np.float32)
    by_word = np.ascontiguousarray(scaled.reshape(k // 512, 128, 4, n).transpose(0, 1, 3, 2))
    if fmt == "e4m3":
        words = by_word.astype(ml_dtypes.float8_e4m3fn).view(np.uint8)
    else:
        c = by_word.astype(ml_dtypes.float4_e2m1fn).view(np.uint8) & 0xF
        words = c[..., 0::2] | (c[..., 1::2] << 4)
    return np.ascontiguousarray(words), np.ascontiguousarray(byte.astype(np.uint8).reshape(k // 512, 16, n))


def unpack_weight(words, scales, fmt):
    g, p, n, _ = words.shape
    if fmt == "e4m3":
        vals = np.ascontiguousarray(words).view(ml_dtypes.float8_e4m3fn).astype(np.float64)
    else:
        nib = np.empty((g, p, n, 4), np.uint8)
        nib[..., 0::2] = words & 0xF
        nib[..., 1::2] = words >> 4
        vals = E2M1[nib]
    vals = vals * np.repeat(np.exp2(scales.astype(np.float64) - 127.0), 8, axis=1)[..., None]
    return vals.transpose(0, 1, 3, 2).reshape(g * 512, n)
def pack4(w):
    words, scales = pack_weight(w, "e2m1")
    return words.reshape(words.shape[0], 128, -1), scales


def unpack4(words, scales):
    return unpack_weight(words.reshape(words.shape[0], 128, -1, 2), scales, "e2m1")


def planes(Y):
    n, m = Y.shape
    b = f64(bf(Y)).reshape(n // 32, 32, m)
    amax = np.abs(b).max(1)
    byte = np.clip(np.where(amax > 0, np.frexp(amax)[1] - 1 + 127 - 7, 1), 1, 254)
    codes = (b * np.exp2(127.0 - byte)[:, None, :]).reshape(n, m).astype(np.float32).astype(ml_dtypes.float8_e4m3fn).view(np.uint8)
    words = codes.reshape(n // 512, 128, 4, m).transpose(0, 1, 3, 2)
    return np.ascontiguousarray(words), np.ascontiguousarray(byte.astype(np.uint8).reshape(n // 512, 16, m))


N, F, D, M = 1024, 1024, 1024, 1024


def setup_inputs():
    p, q = mx_kscale(F), mx_kscale(D)
    x = bf(np.random.standard_normal((N, F)) * p)
    w_words, w_scales = pack4(np.random.standard_normal((F, D)) / np.sqrt(F) / p[:, None])
    c = bf(0.5 * np.random.standard_normal(D))
    g = bf((1.0 + 0.1 * np.random.standard_normal(D)) * q)
    a_words, a_scales = pack4(1.5 * np.random.standard_normal((D, M)) / np.sqrt(D) / q[:, None])
    s = bf(np.random.uniform(0.5, 2.0, M))
    return {"x": x, "w_words": w_words, "w_scales": w_scales, "c": c, "g": g, "a_words": a_words, "a_scales": a_scales, "s": s}


def _embed(x, w_words, w_scales, c, g):
    h = mxq(f64(x), 1, "e4m3") @ unpack4(w_words, w_scales)
    return np.tanh(h + f64(c)[None, :]) * f64(g)[None, :]


def core(x, w_words, w_scales, c, g, a_words, a_scales, s):
    z = _embed(x, w_words, w_scales, c, g)
    t = mxq(z, 1, "e4m3") @ unpack4(a_words, a_scales)
    sk = f64(s)
    u = sk[None, :] * t
    cos_u = np.cos(u)
    sin_u = np.sin(u)
    mc = np.mean(cos_u, axis=0)
    ms = np.mean(sin_u, axis=0)
    psi = np.exp(-sk * sk / 2.0)
    return 4.0 * sk[None, :] * (ms[None, :] * cos_u - (mc - psi)[None, :] * sin_u)


def reference(x, w_words, w_scales, c, g, a_words, a_scales, s):
    R_out = core(x, w_words, w_scales, c, g, a_words, a_scales, s)
    words, scales = planes(R_out)
    return R_out, words, scales

@@ -1,0 +1,364 @@
+from contextlib import ExitStack
+import math
+
+import concourse.mybir as mybir
+from concourse.masks import make_identity
+
+F32 = mybir.dt.float32
+BF16 = mybir.dt.bfloat16
+I32 = mybir.dt.int32
+U32 = mybir.dt.uint32
+U8 = mybir.dt.uint8
+E4M3 = mybir.dt.float8_e4m3fn_x4
+E2M1 = mybir.dt.float4_e2m1fn_x4
+AF = mybir.ActivationFunctionType
+ALU = mybir.AluOpType
+
+P = 128
+N, F, D, M = 1024, 1024, 1024, 1024
+FLOPS = 2 * N * F * D + 2 * N * D * M
+HALF = 512
+MT = M // P
+
+
+def tile_lejepasigregrandomknotslicegrad_x2_kernel(
+    tc, x, w_words, w_scales, c, g, a_words, a_scales, s, out_0, out_1, out_2
+):
+    nc = tc.nc
+    with ExitStack() as ctx:
+        keep = ctx.enter_context(tc.tile_pool(name="keep", bufs=1))
+        work = ctx.enter_context(tc.tile_pool(name="work", bufs=2))
+        psum = ctx.enter_context(tc.psum_pool(name="psum", bufs=1))
+
+        ident = keep.tile([P, P], F32, name="ident")
+        zero = keep.tile([P, 1], F32, name="zero")
+        silu0 = keep.tile([P, 1], F32, name="silu0")
+        nc.vector.memset(zero[:], 0.0)
+        nc.scalar.activation(out=silu0[:], in_=zero[:], func=AF.Silu)
+
+        w_raw = keep.tile([P, 2, 2048], U8, name="w_raw", align_bytes=64)
+        w_sraw = keep.tile([P, 2, 1024], U8, name="w_sraw", align_bytes=64)
+        w_ord = keep.tile([P, 2, 2048], U8, name="w_ord", align_bytes=64)
+        w_sord = keep.tile([P, 2, 1024], U8, name="w_sord", align_bytes=64)
+        a_raw = keep.tile([P, 2, 2048], U8, name="a_raw", align_bytes=64)
+        a_s = keep.tile([P, 2, 1024], U8, name="a_s", align_bytes=64)
+        x_raw = [keep.tile([P, 4, F], BF16, name="x_raw%d" % G, align_bytes=64) for G in range(2)]
+        c_col = keep.tile([P, 2, 4], BF16, name="c_col")
+        g_col = keep.tile([P, 2, 4], BF16, name="g_col")
+        s_row = keep.tile([8, P], BF16, name="s_row")
+        s_pad = keep.tile([P, P], F32, name="s_pad")
+
+        nc.vector.memset(w_sraw[:].rearrange("p g n -> p (g n)").bitcast(I32), 0)
+        nc.gpsimd.memset(s_pad[:], 0.0)
+        make_identity(nc, ident[:])
+        nc.gpsimd.memset(a_s[:].rearrange("p g n -> p (g n)").bitcast(I32), 0)
+
+        w_in = w_words.rearrange("g p n -> p g n")
+        a_in = a_words.rearrange("g p n -> p g n")
+
+        def load_w(h):
+            nc.sync.dma_start(
+                out=w_raw[:, :, 1024 * h : 1024 * h + 1024].bitcast(I32),
+                in_=w_in[:, :, 1024 * h : 1024 * h + 1024].bitcast(I32),
+            )
+
+        def load_scales(dst, src):
+            for Q in range(4):
+                nc.sync.dma_start(
+                    out=dst[32 * Q : 32 * Q + 4, :, :].bitcast(I32),
+                    in_=src[:, 4 * Q : 4 * Q + 4, :].rearrange("g r n -> r g n").bitcast(I32),
+                )
+
+        x_in = x.rearrange("(G p t) f -> G p t f", G=2, t=4)
+
+        def load_x(G, j):
+            nc.sync.dma_start(out=x_raw[G][:, 2 * j : 2 * j + 2, :], in_=x_in[G][:, 2 * j : 2 * j + 2, :])
+
+        def order_w(h):
+            for gk in range(2):
+                nc.vector.tensor_copy(
+                    out=w_ord[:, gk, 1024 * h : 1024 * h + 1024].rearrange("p (t m b) -> p t m b", t=4, b=2),
+                    in_=w_raw[:, gk, 1024 * h : 1024 * h + 1024].rearrange("p (m t b) -> p t m b", t=4, b=2),
+                )
+            nc.vector.tensor_copy(
+                out=w_sord[:, :, 512 * h : 512 * h + 512].rearrange("p g (t m) -> p g t m", t=4),
+                in_=w_sraw[:, :, 512 * h : 512 * h + 512].rearrange("p g (m t) -> p g t m", t=4),
+            )
+
+        x_bf = [[keep.tile([P, 2048], BF16, name="x_bf%d%d" % (G, gk), align_bytes=64) for gk in range(2)] for G in range(2)]
+        x_q = [[keep.tile([P, HALF], U32, name="x_q%d%d" % (G, gk), align_bytes=64) for gk in range(2)] for G in range(2)]
+        x_s = [[keep.tile([P, HALF], U8, name="x_s%d%d" % (G, gk), align_bytes=64) for gk in range(2)] for G in range(2)]
+
+        xt = {}
+
+        def turn_x(G, j, gk):
+            bank = psum.tile([P, 2, 2, P], F32, tag="yb", bufs=4, name="xt")
+            words = x_raw[G][:].rearrange("p t f -> p (t f)").bitcast(F32)
+            for i in range(2):
+                for u in range(2):
+                    first = 512 * (2 * j + i) + 256 * gk + u
+                    nc.tensor.transpose(bank[:, i, u, :], words[:, first : first + 256 - u : 2], ident[:])
+            xt[G, j, gk] = bank
+
+        def copy_x(G, j, gk, on_vector):
+            dst = x_bf[G][gk][:].bitcast(F32).rearrange("q (t r u) -> q t r u", t=4, u=2)[:, 2 * j : 2 * j + 2]
+            src = xt[G, j, gk][:].rearrange("q i u r -> q i r u")
+            if on_vector:
+                nc.vector.tensor_copy(out=dst, in_=src)
+            else:
+                nc.scalar.copy(out=dst, in_=src)
+
+        def quant_x(G, j, gk):
+            cols = slice(256 * j, 256 * j + 256)
+            nc.vector.quantize_mx(
+                out=x_q[G][gk][:, cols].bitcast(E4M3),
+                scales=x_s[G][gk][:, cols],
+                in_=x_bf[G][gk][:, 1024 * j : 1024 * j + 1024],
+            )
+
+        z_q = [[keep.tile([P, HALF], U32, name="z_q%d%d" % (G, h), align_bytes=64) for h in range(2)] for G in range(2)]
+        z_s = [[keep.tile([P, HALF], U8, name="z_s%d%d" % (G, h), align_bytes=64) for h in range(2)] for G in range(2)]
+        th = {}
+        zb = {}
+        hb = {}
+
+        def stage1(G, h, t):
+            hb[G, h, t] = psum.tile([P, HALF], F32, tag="mm", bufs=4, name="hb")
+            for gk in range(2):
+                nc.tensor.matmul_mx(
+                    out=hb[G, h, t][:],
+                    lhsT=w_ord[:, gk, 1024 * h + 256 * t : 1024 * h + 256 * t + 256].bitcast(E2M1),
+                    lhsT_scale=w_sord[:, gk, 512 * h + 128 * t : 512 * h + 128 * t + 128],
+                    rhs=x_q[G][gk][:].bitcast(E4M3),
+                    rhs_scale=x_s[G][gk][:],
+                    start=(gk == 0),
+                    stop=(gk == 1),
+                )
+
+        def squash(G, h, t):
+            if t == 0:
+                th[G, h] = work.tile([P, 4, HALF], F32, tag="th", bufs=3, name="th")
+            nc.scalar.activation(out=th[G, h][:, t, :], in_=hb[G, h, t][:], func=AF.Tanh, bias=c_col[:, h, t : t + 1])
+
+        def gain(G, h):
+            zb[G, h] = work.tile([P, HALF, 4], BF16, tag="zb", bufs=2, name="zb", align_bytes=64)
+            nc.vector.tensor_tensor(
+                out=zb[G, h][:],
+                in0=th[G, h][:].rearrange("p t n -> p n t"),
+                in1=g_col[:, h, :].unsqueeze(1).to_broadcast([P, HALF, 4]),
+                op=ALU.mult,
+            )
+
+        def quant_z(G, h):
+            nc.vector.quantize_mx(
+                out=z_q[G][h][:].bitcast(E4M3), scales=z_s[G][h][:], in_=zb[G, h][:].rearrange("p n t -> p (n t)")
+            )
+
+        sc = keep.tile([P, MT], F32, name="sc")
+        turns = keep.tile([P, MT], F32, name="turns")
+        sq = keep.tile([P, MT], F32, name="sq")
+        th_s = keep.tile([P, MT], F32, name="th_s")
+        den = keep.tile([P, MT], F32, name="den")
+        rec = keep.tile([P, MT], F32, name="rec")
+        num = keep.tile([P, MT], F32, name="num")
+        b0 = keep.tile([P, MT], F32, name="b0")
+        co_a = keep.tile([P, MT, 2], F32, name="co_a")
+        co_b = keep.tile([P, MT], F32, name="co_b")
+
+        def knots_a():
+            nc.vector.tensor_copy(out=s_pad[0:8, :], in_=s_row[:])
+            s_bank = psum.tile([P, P], F32, tag="mm", bufs=4, name="s_bank")
+            nc.tensor.transpose(s_bank[:], s_pad[:], ident[:])
+            nc.vector.tensor_copy(out=sc[:], in_=s_bank[:, 0:MT])
+            nc.vector.tensor_scalar(out=turns[:], in0=sc[:], scalar1=1.0 / (2.0 * math.pi), scalar2=None, op0=ALU.mult)
+            nc.gpsimd.tensor_tensor(out=sq[:], in0=sc[:], in1=sc[:], op=ALU.mult)
+            nc.gpsimd.tensor_scalar(out=co_a[:, :, 0], in0=sc[:], scalar1=4.0 / N, scalar2=0.0, op0=ALU.mult, op1=ALU.add)
+            nc.gpsimd.tensor_scalar(out=co_a[:, :, 1], in0=sc[:], scalar1=-8.0 / N, scalar2=0.0, op0=ALU.mult, op1=ALU.add)
+            nc.gpsimd.tensor_scalar(out=co_b[:], in0=sc[:], scalar1=8.0 / N, scalar2=0.0, op0=ALU.mult, op1=ALU.add)
+
+        def knots_b():
+            nc.scalar.activation(out=th_s[:], in_=sq[:], func=AF.Tanh, scale=0.25, bias=silu0[:])
+            nc.gpsimd.tensor_scalar(out=den[:], in0=th_s[:], scalar1=1.0, scalar2=0.0, op0=ALU.add, op1=ALU.add)
+            nc.gpsimd.tensor_tensor(out=num[:], in0=th_s[:], in1=sc[:], op=ALU.mult)
+
+        def knots_c():
+            nc.vector.reciprocal(out=rec[:], in_=den[:])
+            nc.vector.scalar_tensor_tensor(out=b0[:], in0=num[:], scalar=-8.0, in1=rec[:], op0=ALU.mult, op1=ALU.mult)
+
+        y_s = keep.tile([P, 2, M], U8, name="y_s", align_bytes=64)
+        out_rows = out_0.rearrange("(G p t) m -> G p t m", G=2, t=4)
+        out_words = out_1.rearrange("G p m t -> G p (m t)")
+
+        tb = {}
+        k_t = {}
+        f_t = {}
+        sums = {}
+        sin_u = {}
+        sin_h = {}
+        sq_h = {}
+        yb = {}
+        r = {}
+        y_bf = {}
+        y_q = {}
+
+        def stage2(m, G):
+            tb[m, G] = psum.tile([P, HALF], F32, tag="mm", bufs=4, name="tb")
+            for h in range(2):
+                nc.tensor.matmul_mx(
+                    out=tb[m, G][:],
+                    lhsT=a_raw[:, h, 256 * m : 256 * m + 256].bitcast(E2M1),
+                    lhsT_scale=a_s[:, h, 128 * m : 128 * m + 128],
+                    rhs=z_q[G][h][:].bitcast(E4M3),
+                    rhs_scale=z_s[G][h][:],
+                    start=(h == 0),
+                    stop=(h == 1),
+                )
+
+        def whole(m, G):
+            k_t[m, G] = work.tile([P, HALF], I32, tag="k_t", bufs=4, name="k_t")
+            nc.vector.tensor_scalar(out=k_t[m, G][:], in0=tb[m, G][:], scalar1=turns[:, m : m + 1], scalar2=None, op0=ALU.mult)
+
+        def rest(m, G):
+            if m not in f_t:
+                f_t[m] = work.tile([P, N], F32, tag="f_t", bufs=5, name="f_t")
+            nc.vector.scalar_tensor_tensor(
+                out=f_t[m][:, HALF * G : HALF * G + HALF], in0=tb[m, G][:], scalar=turns[:, m : m + 1], in1=k_t[m, G][:], op0=ALU.mult, op1=ALU.subtract
+            )
+
+        def waves(m, part, parts):
+            width = N // parts
+            cols = slice(width * part, width * part + width)
+            if part == 0:
+                sums[m] = work.tile([P, 2, 2], F32, tag="sums", bufs=5, name="sums")
+                sin_u[m] = work.tile([P, N], F32, tag="sin_u", bufs=6, name="sin_u")
+                sq_h[m] = work.tile([P, N], F32, tag="sq_h", bufs=6, name="sq_h")
+            sin_h = work.tile([P, N], F32, tag="sin_h", bufs=2, name="sin_h")
+            nc.scalar.activation(out=sin_u[m][:, cols], in_=f_t[m][:, cols], func=AF.Sin, scale=2.0 * math.pi, accum_out=sums[m][:, part, 0:1])
+            nc.scalar.activation(out=sin_h[:, cols], in_=f_t[m][:, cols], func=AF.Sin, scale=math.pi)
+            nc.scalar.activation(out=sq_h[m][:, cols], in_=sin_h[:, cols], func=AF.Square, accum_out=sums[m][:, part, 1:2])
+
+        def terms(m, parts, eng):
+            if parts == 2:
+                nc.gpsimd.tensor_tensor(out=sums[m][:, 0, :], in0=sums[m][:, 0, :], in1=sums[m][:, 1, :], op=ALU.add)
+            ab = work.tile([P, 3], F32, tag="ab", bufs=3, name="ab")
+            nc.gpsimd.tensor_scalar(out=ab[:, 0:2], in0=co_a[:, m, :], scalar1=sums[m][:, 0, 0:1], scalar2=0.0, op0=ALU.mult, op1=ALU.add)
+            nc.gpsimd.tensor_scalar(out=ab[:, 2:3], in0=sums[m][:, 0, 1:2], scalar1=co_b[:, m : m + 1], scalar2=b0[:, m : m + 1], op0=ALU.mult, op1=ALU.add)
+            for G in range(2):
+                cols = slice(HALF * G, HALF * G + HALF)
+                eng.tensor_scalar(out=sq_h[m][:, cols], in0=sq_h[m][:, cols], scalar1=ab[:, 1:2], scalar2=ab[:, 0:1], op0=ALU.mult, op1=ALU.add)
+                eng.tensor_scalar(out=sin_u[m][:, cols], in0=sin_u[m][:, cols], scalar1=ab[:, 2:3], scalar2=0.0, op0=ALU.mult, op1=ALU.add)
+
+        def turn_y(m, G):
+            yb[m, G] = psum.tile([P, 4, P], F32, tag="yb", bufs=4, name="yb")
+            for t in range(4):
+                cols = slice(HALF * G + P * t, HALF * G + P * t + P)
+                nc.tensor.matmul(yb[m, G][:, t, :], lhsT=sq_h[m][:, cols], rhs=ident[:], is_transpose=True, start=True, stop=False)
+                nc.tensor.matmul(yb[m, G][:, t, :], lhsT=sin_u[m][:, cols], rhs=ident[:], is_transpose=True, start=False, stop=True)
+
+        def empty_y(m, G, on_scalar):
+            if m % 2 == 0:
+                r[m // 2, G] = work.tile([P, 4, 2 * P], F32, tag="r%d" % G, bufs=3, name="r%d" % G)
+            dst = r[m // 2, G][:, :, P * (m % 2) : P * (m % 2) + P]
+            if on_scalar:
+                nc.scalar.copy(out=dst, in_=yb[m, G][:])
+            else:
+                nc.vector.tensor_copy(out=dst, in_=yb[m, G][:])
+
+        def store_rows(b, G):
+            nc.sync.dma_start(out=out_rows[G][:, :, 256 * b : 256 * b + 256], in_=r[b, G][:])
+
+        def lay_y(m, G):
+            y_bf[m, G] = work.tile([P, P, 4], BF16, tag="y_bf", bufs=4, name="y_bf", align_bytes=64)
+            nc.vector.tensor_copy(out=y_bf[m, G][:], in_=r[m // 2, G][:, :, P * (m % 2) : P * (m % 2) + P].rearrange("p t m -> p m t"))
+
+        def quant_y(m, G):
+            if m % 2 == 0:
+                y_q[m // 2, G] = work.tile([P, 2 * P], U32, tag="y_q%d" % G, bufs=2, name="y_q%d" % G, align_bytes=64)
+            nc.vector.quantize_mx(
+                out=y_q[m // 2, G][:, P * (m % 2) : P * (m % 2) + P].bitcast(E4M3),
+                scales=y_s[:, G, P * m : P * m + P],
+                in_=y_bf[m, G][:].rearrange("p m t -> p (m t)"),
+            )
+
+        def store_words(b, G):
+            nc.sync.dma_start(out=out_words[G][:, 1024 * b : 1024 * b + 1024].bitcast(I32), in_=y_q[b, G][:].bitcast(I32))
+
+        plan = []
+
+        def at(slot, step, *args):
+            plan.append((slot, len(plan), step, args))
+
+        load_x(0, 0)
+        load_x(0, 1)
+        load_w(0)
+        load_scales(w_sraw, w_scales)
+        load_x(1, 0)
+        nc.sync.dma_start(out=c_col[:], in_=c.rearrange("(g p t) -> p g t", g=2, t=4))
+        nc.sync.dma_start(out=g_col[:], in_=g.rearrange("(g p t) -> p g t", g=2, t=4))
+        load_w(1)
+        load_x(1, 1)
+        nc.sync.dma_start(out=s_row[:], in_=s.rearrange("(j p) -> j p", p=P))
+        nc.sync.dma_start(out=a_raw[:].bitcast(I32), in_=a_in.bitcast(I32))
+        load_scales(a_s, a_scales)
+
+        for G in range(2):
+            for j in range(2):
+                for gk in range(2):
+                    at([[-0.9,2.14],[3.89,8.64]][G][j] , turn_x, G, j, gk)
+                    at([[3.57,4.86],[4.88,9.18]][G][j], copy_x, G, j, gk, [0,0][G] == 1)
+                    at([[4.85,6.73],[9.63,9.84]][G][j], quant_x, G, j, gk)
+        at([3.71,8.2][0], order_w, 0)
+        at([3.71,8.2][1], order_w, 1)
+        for G in range(2):
+            for h in range(2):
+                for t in range(4):
+                    at([[6.91,8.31],[10.53,12.59]][G][h] + 0.4 * t, stage1, G, h, t)
+                    at([[7.16,9.45],[10.94,14.92]][G][h] + 0.4 * t, squash, G, h, t)
+                at([[8.69,11.85],[12.34,17]][G][h], gain, G, h)
+                at([[8.69,11.85],[12.34,17]][G][h] + 2.77, quant_z, G, h)
+        at([8.57,8.95,10.35][0], knots_a)
+        at([8.57,8.95,10.35][1], knots_b)
+        at([8.57,8.95,10.35][2], knots_c)
+        for m in range(MT):
+            split = m < 2
+            if split:
+                fronts = [17.54 + 1.46 * m, 21.15 + 2.73 * m]
+            else:
+                fronts = [25.22 + 2.36 * (m - 2)] * 2
+            for G in range(2):
+                at(fronts[G] - 1.31, stage2, m, G)
+            for G in range(2):
+                at(fronts[G], whole, m, G)
+            for G in range(2):
+                at(fronts[G] + 0.01, rest, m, G)
+            if split:
+                at(fronts[0] + 0.57, waves, m, 0, 2)
+                at(fronts[1] + 0.57, waves, m, 1, 2)
+            else:
+                at(fronts[1] + 0.57, waves, m, 0, 1)
+            last = max(fronts)
+            on_vector = m in [7, 6, 3]
+            at(last + 5.4, terms, m, 2 if split else 1, nc.vector if on_vector else nc.gpsimd)
+            for G in range(2):
+                at(last + 6.67, turn_y, m, G)
+            for G in range(2):
+                at(last + 7.19, empty_y, m, G, (m, G) in [(2, 1), (4, 0), (6, 1), (7, 1), (7, 0), (6, 0)])
+            if m % 2:
+                for G in range(2):
+                    at(last + 7.19, store_rows, m // 2, G)
+            for G in range(2):
+                at(last + 14.82, lay_y, m, G)
+            for G in range(2):
+                at(last + 14.82 + 0.01, quant_y, m, G)
+            if m % 2:
+                for G in range(2):
+                    at(last + 14.82 + 0.02, store_words, m // 2, G)
+        with tc.manual_schedule():
+            for slot, tie, step, args in sorted(plan):
+                step(*args)
+
+        for Q in range(4):
+            nc.sync.dma_start(
+                out=out_2[:, 4 * Q : 4 * Q + 4, :].rearrange("g r m -> r g m").bitcast(I32),
+                in_=y_s[32 * Q : 32 * Q + 4, :, :].bitcast(I32),
+            )

@@ -143,9 +143,9 @@ def tile_lejepasigregrandomknotslicegrad_x2_kernel(
         def gain(G, h):
             zb[G, h] = work.tile([P, HALF, 4], BF16, tag="zb", bufs=2, name="zb", align_bytes=64)
             nc.vector.tensor_tensor(
-                out=zb[G, h][:],
-                in0=th[G, h][:].rearrange("p t n -> p n t"),
-                in1=g_col[:, h, :].unsqueeze(1).to_broadcast([P, HALF, 4]),
+                out=zb[G, h][:].rearrange("p (b i) t -> p b t i", i=4),
+                in0=th[G, h][:].rearrange("p t (b i) -> p b t i", i=4),
+                in1=g_col[:, h, :].unsqueeze(1).unsqueeze(3).to_broadcast([P, HALF // 4, 4, 4]),
                 op=ALU.mult,
             )
 
@@ -269,7 +269,10 @@ def tile_lejepasigregrandomknotslicegrad_x2_kernel(
 
         def lay_y(m, G):
             y_bf[m, G] = work.tile([P, P, 4], BF16, tag="y_bf", bufs=4, name="y_bf", align_bytes=64)
-            nc.vector.tensor_copy(out=y_bf[m, G][:], in_=r[m // 2, G][:, :, P * (m % 2) : P * (m % 2) + P].rearrange("p t m -> p m t"))
+            nc.vector.tensor_copy(
+                out=y_bf[m, G][:].rearrange("p (b i) t -> p b t i", i=4),
+                in_=r[m // 2, G][:, :, P * (m % 2) : P * (m % 2) + P].rearrange("p t (b i) -> p b t i", i=4),
+            )
 
         def quant_y(m, G):
             if m % 2 == 0:
@@ -288,13 +291,13 @@ def tile_lejepasigregrandomknotslicegrad_x2_kernel(
         def at(slot, step, *args):
             plan.append((slot, len(plan), step, args))
 
-        load_x(0, 0)
-        load_x(0, 1)
-        load_w(0)
         load_scales(w_sraw, w_scales)
-        load_x(1, 0)
+        load_x(0, 0)
+        load_w(0)
+        load_x(0, 1)
         nc.sync.dma_start(out=c_col[:], in_=c.rearrange("(g p t) -> p g t", g=2, t=4))
         nc.sync.dma_start(out=g_col[:], in_=g.rearrange("(g p t) -> p g t", g=2, t=4))
+        load_x(1, 0)
         load_w(1)
         load_x(1, 1)
         nc.sync.dma_start(out=s_row[:], in_=s.rearrange("(j p) -> j p", p=P))
@@ -304,55 +307,55 @@ def tile_lejepasigregrandomknotslicegrad_x2_kernel(
         for G in range(2):
             for j in range(2):
                 for gk in range(2):
-                    at([[-0.9,2.14],[3.89,8.64]][G][j] , turn_x, G, j, gk)
-                    at([[3.57,4.86],[4.88,9.18]][G][j], copy_x, G, j, gk, [0,0][G] == 1)
-                    at([[4.85,6.73],[9.63,9.84]][G][j], quant_x, G, j, gk)
-        at([3.71,8.2][0], order_w, 0)
-        at([3.71,8.2][1], order_w, 1)
+                    at([[-1,0],[4.21,9.29]][G][j] , turn_x, G, j, gk)
+                    at([[4.2,5.2],[5.9,9.31]][G][j], copy_x, G, j, gk, [0,0][G] == 1)
+                    at([[5.5,6.5],[8.27,9.88]][G][j], quant_x, G, j, gk)
+        at([4.8,7][0], order_w, 0)
+        at([4.8,7][1], order_w, 1)
         for G in range(2):
             for h in range(2):
                 for t in range(4):
-                    at([[6.91,8.31],[10.53,12.59]][G][h] + 0.4 * t, stage1, G, h, t)
-                    at([[7.16,9.45],[10.94,14.92]][G][h] + 0.4 * t, squash, G, h, t)
-                at([[8.69,11.85],[12.34,17]][G][h], gain, G, h)
-                at([[8.69,11.85],[12.34,17]][G][h] + 2.77, quant_z, G, h)
-        at([8.57,8.95,10.35][0], knots_a)
-        at([8.57,8.95,10.35][1], knots_b)
-        at([8.57,8.95,10.35][2], knots_c)
+                    at([[7.41,8.8],[10.25,11.82]][G][h] + 0.4 * t, stage1, G, h, t)
+                    at([[7.47,8.85],[10.94,13.19]][G][h] + 0.4 * t, squash, G, h, t)
+                at([[9.47,12.85],[14.84,15.52]][G][h], gain, G, h)
+                at([[9.47,12.85],[14.84,15.52]][G][h] + 0.91, quant_z, G, h)
+        at([9.07,9.43,11.69][0], knots_a)
+        at([9.07,9.43,11.69][1], knots_b)
+        at([9.07,9.43,11.69][2], knots_c)
         for m in range(MT):
             split = m < 2
             if split:
-                fronts = [17.54 + 1.46 * m, 21.15 + 2.73 * m]
+                fronts = [17.73 + -1.98 * m, 22.12 + 3.8 * m]
             else:
-                fronts = [25.22 + 2.36 * (m - 2)] * 2
+                fronts = [26.82 + 2.12 * (m - 2)] * 2
             for G in range(2):
-                at(fronts[G] - 1.31, stage2, m, G)
+                at(fronts[G] - 0.82, stage2, m, G)
             for G in range(2):
                 at(fronts[G], whole, m, G)
             for G in range(2):
                 at(fronts[G] + 0.01, rest, m, G)
             if split:
-                at(fronts[0] + 0.57, waves, m, 0, 2)
-                at(fronts[1] + 0.57, waves, m, 1, 2)
+                at(fronts[0] + 2.42, waves, m, 0, 2)
+                at(fronts[1] + 2.42, waves, m, 1, 2)
             else:
-                at(fronts[1] + 0.57, waves, m, 0, 1)
+                at(fronts[1] + 2.42, waves, m, 0, 1)
             last = max(fronts)
-            on_vector = m in [7, 6, 3]
-            at(last + 5.4, terms, m, 2 if split else 1, nc.vector if on_vector else nc.gpsimd)
+            on_vector = m in [0, 1, 2, 3, 4, 5, 6, 7]
+            at(last + 5.08, terms, m, 2 if split else 1, nc.vector if on_vector else nc.gpsimd)
             for G in range(2):
-                at(last + 6.67, turn_y, m, G)
+                at(last + 6.53, turn_y, m, G)
             for G in range(2):
-                at(last + 7.19, empty_y, m, G, (m, G) in [(2, 1), (4, 0), (6, 1), (7, 1), (7, 0), (6, 0)])
+                at(last + 7.66, empty_y, m, G, (m, G) in [(3, 1), (4, 0), (6, 0), (6, 1), (1, 1), (2, 1), (0, 0), (3, 0), (5, 1), (7, 0), (0, 1), (7, 1)])
             if m % 2:
                 for G in range(2):
-                    at(last + 7.19, store_rows, m // 2, G)
+                    at(last + 7.66, store_rows, m // 2, G)
             for G in range(2):
-                at(last + 14.82, lay_y, m, G)
+                at(last + 9.78, lay_y, m, G)
             for G in range(2):
-                at(last + 14.82 + 0.01, quant_y, m, G)
+                at(last + 9.78 + 0.01, quant_y, m, G)
             if m % 2:
                 for G in range(2):
-                    at(last + 14.82 + 0.02, store_words, m // 2, G)
+                    at(last + 9.78 + 0.02, store_words, m // 2, G)
         with tc.manual_schedule():
             for slot, tie, step, args in sorted(plan):
                 step(*args)

@@ -19,6 +19,8 @@ N, F, D, M = 1024, 1024, 1024, 1024
 FLOPS = 2 * N * F * D + 2 * N * D * M
 HALF = 512
 MT = M // P
+TURN_SPLIT = 11.0
+ON_TENSOR = (2, 4, 5, 3)
 
 
 def tile_lejepasigregrandomknotslicegrad_x2_kernel(
@@ -35,6 +37,8 @@ def tile_lejepasigregrandomknotslicegrad_x2_kernel(
         silu0 = keep.tile([P, 1], F32, name="silu0")
         nc.vector.memset(zero[:], 0.0)
         nc.scalar.activation(out=silu0[:], in_=zero[:], func=AF.Silu)
+        two_pi = keep.tile([P, 1], F32, name="two_pi")
+        nc.vector.tensor_scalar(out=two_pi[:], in0=zero[:], scalar1=2.0 * math.pi / TURN_SPLIT, scalar2=TURN_SPLIT, op0=ALU.add, op1=ALU.mult)
 
         w_raw = keep.tile([P, 2, 2048], U8, name="w_raw", align_bytes=64)
         w_sraw = keep.tile([P, 2, 1024], U8, name="w_sraw", align_bytes=64)
@@ -44,14 +48,15 @@ def tile_lejepasigregrandomknotslicegrad_x2_kernel(
         a_s = keep.tile([P, 2, 1024], U8, name="a_s", align_bytes=64)
         x_raw = [keep.tile([P, 4, F], BF16, name="x_raw%d" % G, align_bytes=64) for G in range(2)]
         c_col = keep.tile([P, 2, 4], BF16, name="c_col")
+        g_f32 = keep.tile([P, 2, 4], F32, name="g_f32")
         g_col = keep.tile([P, 2, 4], BF16, name="g_col")
         s_row = keep.tile([8, P], BF16, name="s_row")
         s_pad = keep.tile([P, P], F32, name="s_pad")
 
         nc.vector.memset(w_sraw[:].rearrange("p g n -> p (g n)").bitcast(I32), 0)
-        nc.gpsimd.memset(s_pad[:], 0.0)
         make_identity(nc, ident[:])
-        nc.gpsimd.memset(a_s[:].rearrange("p g n -> p (g n)").bitcast(I32), 0)
+        nc.vector.memset(s_pad[:], 0.0)
+        nc.vector.memset(a_s[:].rearrange("p g n -> p (g n)").bitcast(I32), 0)
 
         w_in = w_words.rearrange("g p n -> p g n")
         a_in = a_words.rearrange("g p n -> p g n")
@@ -62,17 +67,18 @@ def tile_lejepasigregrandomknotslicegrad_x2_kernel(
                 in_=w_in[:, :, 1024 * h : 1024 * h + 1024].bitcast(I32),
             )
 
-        def load_scales(dst, src):
+        def load_scales(queue, dst, src):
             for Q in range(4):
-                nc.sync.dma_start(
+                queue.dma_start(
                     out=dst[32 * Q : 32 * Q + 4, :, :].bitcast(I32),
                     in_=src[:, 4 * Q : 4 * Q + 4, :].rearrange("g r n -> r g n").bitcast(I32),
                 )
 
         x_in = x.rearrange("(G p t) f -> G p t f", G=2, t=4)
 
-        def load_x(G, j):
-            nc.sync.dma_start(out=x_raw[G][:, 2 * j : 2 * j + 2, :], in_=x_in[G][:, 2 * j : 2 * j + 2, :])
+        def load_x(G, first, count):
+            slots = slice(first, first + count)
+            nc.sync.dma_start(out=x_raw[G][:, slots, :], in_=x_in[G][:, slots, :])
 
         def order_w(h):
             for gk in range(2):
@@ -122,32 +128,52 @@ def tile_lejepasigregrandomknotslicegrad_x2_kernel(
         zb = {}
         hb = {}
 
-        def stage1(G, h, t):
-            hb[G, h, t] = psum.tile([P, HALF], F32, tag="mm", bufs=4, name="hb")
-            for gk in range(2):
-                nc.tensor.matmul_mx(
-                    out=hb[G, h, t][:],
-                    lhsT=w_ord[:, gk, 1024 * h + 256 * t : 1024 * h + 256 * t + 256].bitcast(E2M1),
-                    lhsT_scale=w_sord[:, gk, 512 * h + 128 * t : 512 * h + 128 * t + 128],
-                    rhs=x_q[G][gk][:].bitcast(E4M3),
-                    rhs_scale=x_s[G][gk][:],
-                    start=(gk == 0),
-                    stop=(gk == 1),
-                )
+        def stage1(G, h, t, part, parts):
+            hb[G, h, t, part] = psum.tile([P, HALF], F32, tag="mm", bufs=4, name="hb")
+            width = HALF if parts == 1 else P
+            for first in range(0, HALF // parts, width):
+                cols = slice(HALF // parts * part + first, HALF // parts * part + first + width)
+                for gk in range(2):
+                    nc.tensor.matmul_mx(
+                        out=hb[G, h, t, part][:, first : first + width],
+                        lhsT=w_ord[:, gk, 1024 * h + 256 * t : 1024 * h + 256 * t + 256].bitcast(E2M1),
+                        lhsT_scale=w_sord[:, gk, 512 * h + 128 * t : 512 * h + 128 * t + 128],
+                        rhs=x_q[G][gk][:, cols].bitcast(E4M3),
+                        rhs_scale=x_s[G][gk][:, cols],
+                        start=(gk == 0),
+                        stop=(gk == 1),
+                    )
 
-        def squash(G, h, t):
-            if t == 0:
+        def squash(G, h, t, part, parts):
+            width = HALF // parts
+            if (G, h) not in th:
                 th[G, h] = work.tile([P, 4, HALF], F32, tag="th", bufs=3, name="th")
-            nc.scalar.activation(out=th[G, h][:, t, :], in_=hb[G, h, t][:], func=AF.Tanh, bias=c_col[:, h, t : t + 1])
-
-        def gain(G, h):
-            zb[G, h] = work.tile([P, HALF, 4], BF16, tag="zb", bufs=2, name="zb", align_bytes=64)
-            nc.vector.tensor_tensor(
-                out=zb[G, h][:].rearrange("p (b i) t -> p b t i", i=4),
-                in0=th[G, h][:].rearrange("p t (b i) -> p b t i", i=4),
-                in1=g_col[:, h, :].unsqueeze(1).unsqueeze(3).to_broadcast([P, HALF // 4, 4, 4]),
-                op=ALU.mult,
+            nc.scalar.activation(
+                out=th[G, h][:, t, width * part : width * part + width], in_=hb[G, h, t, part][:, 0:width], func=AF.Tanh, bias=c_col[:, h, t : t + 1]
             )
+
+        zt = {}
+
+        def scale_z(G, h, t):
+            if (G, h) not in zt:
+                zt[G, h] = work.tile([P, 4, HALF], BF16, tag="zt", bufs=1, name="zt")
+            nc.scalar.activation(out=zt[G, h][:, t, :], in_=th[G, h][:, t, :], func=AF.Copy, scale=g_f32[:, h, t : t + 1])
+
+        def gain(G, h, part, parts, scaled):
+            if (G, h) not in zb:
+                zb[G, h] = work.tile([P, HALF, 4], BF16, tag="zb", bufs=2, name="zb", align_bytes=64)
+            width = HALF // parts
+            cols = slice(width * part, width * part + width)
+            dst = zb[G, h][:, cols, :].rearrange("p (b i) t -> p b t i", i=4)
+            if scaled:
+                nc.vector.tensor_copy(out=dst, in_=zt[G, h][:, :, cols].rearrange("p t (b i) -> p b t i", i=4))
+            else:
+                nc.vector.tensor_tensor(
+                    out=dst,
+                    in0=th[G, h][:, :, cols].rearrange("p t (b i) -> p b t i", i=4),
+                    in1=g_col[:, h, :].unsqueeze(1).unsqueeze(3).to_broadcast([P, width // 4, 4, 4]),
+                    op=ALU.mult,
+                )
 
         def quant_z(G, h):
             nc.vector.quantize_mx(
@@ -165,10 +191,21 @@ def tile_lejepasigregrandomknotslicegrad_x2_kernel(
         co_a = keep.tile([P, MT, 2], F32, name="co_a")
         co_b = keep.tile([P, MT], F32, name="co_b")
 
+        knot_bank = []
+
         def knots_a():
             nc.vector.tensor_copy(out=s_pad[0:8, :], in_=s_row[:])
+
+        def knots_t():
             s_bank = psum.tile([P, P], F32, tag="mm", bufs=4, name="s_bank")
             nc.tensor.transpose(s_bank[:], s_pad[:], ident[:])
+            knot_bank.append(s_bank)
+
+        def knots_g():
+            nc.gpsimd.tensor_copy(out=g_f32[:], in_=g_col[:])
+
+        def knots_d():
+            s_bank = knot_bank[0]
             nc.vector.tensor_copy(out=sc[:], in_=s_bank[:, 0:MT])
             nc.vector.tensor_scalar(out=turns[:], in0=sc[:], scalar1=1.0 / (2.0 * math.pi), scalar2=None, op0=ALU.mult)
             nc.gpsimd.tensor_tensor(out=sq[:], in0=sc[:], in1=sc[:], op=ALU.mult)
@@ -228,14 +265,16 @@ def tile_lejepasigregrandomknotslicegrad_x2_kernel(
         def waves(m, part, parts):
             width = N // parts
             cols = slice(width * part, width * part + width)
-            if part == 0:
+            if m not in sums:
                 sums[m] = work.tile([P, 2, 2], F32, tag="sums", bufs=5, name="sums")
                 sin_u[m] = work.tile([P, N], F32, tag="sin_u", bufs=6, name="sin_u")
                 sq_h[m] = work.tile([P, N], F32, tag="sq_h", bufs=6, name="sq_h")
             sin_h = work.tile([P, N], F32, tag="sin_h", bufs=2, name="sin_h")
-            nc.scalar.activation(out=sin_u[m][:, cols], in_=f_t[m][:, cols], func=AF.Sin, scale=2.0 * math.pi, accum_out=sums[m][:, part, 0:1])
+            nc.scalar.activation(out=sin_u[m][:, cols], in_=f_t[m][:, cols], func=AF.Sin, scale=two_pi[:], accum_out=sums[m][:, part, 0:1])
             nc.scalar.activation(out=sin_h[:, cols], in_=f_t[m][:, cols], func=AF.Sin, scale=math.pi)
             nc.scalar.activation(out=sq_h[m][:, cols], in_=sin_h[:, cols], func=AF.Square, accum_out=sums[m][:, part, 1:2])
+
+        diag = {}
 
         def terms(m, parts, eng):
             if parts == 2:
@@ -246,17 +285,24 @@ def tile_lejepasigregrandomknotslicegrad_x2_kernel(
             for G in range(2):
                 cols = slice(HALF * G, HALF * G + HALF)
                 eng.tensor_scalar(out=sq_h[m][:, cols], in0=sq_h[m][:, cols], scalar1=ab[:, 1:2], scalar2=ab[:, 0:1], op0=ALU.mult, op1=ALU.add)
-                eng.tensor_scalar(out=sin_u[m][:, cols], in0=sin_u[m][:, cols], scalar1=ab[:, 2:3], scalar2=0.0, op0=ALU.mult, op1=ALU.add)
+                if m not in ON_TENSOR:
+                    eng.tensor_scalar(out=sin_u[m][:, cols], in0=sin_u[m][:, cols], scalar1=ab[:, 2:3], scalar2=0.0, op0=ALU.mult, op1=ALU.add)
+            if m in ON_TENSOR:
+                diag[m] = work.tile([P, P], F32, tag="diag", bufs=3, name="diag")
+                eng.tensor_scalar(out=diag[m][:], in0=ident[:], scalar1=ab[:, 2:3], scalar2=None, op0=ALU.mult)
 
         def turn_y(m, G):
             yb[m, G] = psum.tile([P, 4, P], F32, tag="yb", bufs=4, name="yb")
             for t in range(4):
                 cols = slice(HALF * G + P * t, HALF * G + P * t + P)
                 nc.tensor.matmul(yb[m, G][:, t, :], lhsT=sq_h[m][:, cols], rhs=ident[:], is_transpose=True, start=True, stop=False)
-                nc.tensor.matmul(yb[m, G][:, t, :], lhsT=sin_u[m][:, cols], rhs=ident[:], is_transpose=True, start=False, stop=True)
+                if m in ON_TENSOR:
+                    nc.tensor.matmul(yb[m, G][:, t, :], lhsT=sin_u[m][:, cols], rhs=diag[m][:], start=False, stop=True)
+                else:
+                    nc.tensor.matmul(yb[m, G][:, t, :], lhsT=sin_u[m][:, cols], rhs=ident[:], is_transpose=True, start=False, stop=True)
 
         def empty_y(m, G, on_scalar):
-            if m % 2 == 0:
+            if (m // 2, G) not in r:
                 r[m // 2, G] = work.tile([P, 4, 2 * P], F32, tag="r%d" % G, bufs=3, name="r%d" % G)
             dst = r[m // 2, G][:, :, P * (m % 2) : P * (m % 2) + P]
             if on_scalar:
@@ -275,7 +321,7 @@ def tile_lejepasigregrandomknotslicegrad_x2_kernel(
             )
 
         def quant_y(m, G):
-            if m % 2 == 0:
+            if (m // 2, G) not in y_q:
                 y_q[m // 2, G] = work.tile([P, 2 * P], U32, tag="y_q%d" % G, bufs=2, name="y_q%d" % G, align_bytes=64)
             nc.vector.quantize_mx(
                 out=y_q[m // 2, G][:, P * (m % 2) : P * (m % 2) + P].bitcast(E4M3),
@@ -286,79 +332,260 @@ def tile_lejepasigregrandomknotslicegrad_x2_kernel(
         def store_words(b, G):
             nc.sync.dma_start(out=out_words[G][:, 1024 * b : 1024 * b + 1024].bitcast(I32), in_=y_q[b, G][:].bitcast(I32))
 
-        plan = []
-
-        def at(slot, step, *args):
-            plan.append((slot, len(plan), step, args))
-
-        load_scales(w_sraw, w_scales)
-        load_x(0, 0)
+        load_scales(nc.sync, w_sraw, w_scales)
+        nc.gpsimd.dma_start(out=c_col[:], in_=c.rearrange("(g p t) -> p g t", g=2, t=4))
+        nc.gpsimd.dma_start(out=g_col[:], in_=g.rearrange("(g p t) -> p g t", g=2, t=4))
+        nc.gpsimd.dma_start(out=s_row[:], in_=s.rearrange("(j p) -> j p", p=P))
+        load_x(0, 0, 2)
         load_w(0)
-        load_x(0, 1)
-        nc.sync.dma_start(out=c_col[:], in_=c.rearrange("(g p t) -> p g t", g=2, t=4))
-        nc.sync.dma_start(out=g_col[:], in_=g.rearrange("(g p t) -> p g t", g=2, t=4))
-        load_x(1, 0)
+        load_x(0, 2, 2)
         load_w(1)
-        load_x(1, 1)
-        nc.sync.dma_start(out=s_row[:], in_=s.rearrange("(j p) -> j p", p=P))
+        load_x(1, 0, 2)
+        load_x(1, 2, 2)
         nc.sync.dma_start(out=a_raw[:].bitcast(I32), in_=a_in.bitcast(I32))
-        load_scales(a_s, a_scales)
-
-        for G in range(2):
-            for j in range(2):
-                for gk in range(2):
-                    at([[-1,0],[4.21,9.29]][G][j] , turn_x, G, j, gk)
-                    at([[4.2,5.2],[5.9,9.31]][G][j], copy_x, G, j, gk, [0,0][G] == 1)
-                    at([[5.5,6.5],[8.27,9.88]][G][j], quant_x, G, j, gk)
-        at([4.8,7][0], order_w, 0)
-        at([4.8,7][1], order_w, 1)
-        for G in range(2):
-            for h in range(2):
-                for t in range(4):
-                    at([[7.41,8.8],[10.25,11.82]][G][h] + 0.4 * t, stage1, G, h, t)
-                    at([[7.47,8.85],[10.94,13.19]][G][h] + 0.4 * t, squash, G, h, t)
-                at([[9.47,12.85],[14.84,15.52]][G][h], gain, G, h)
-                at([[9.47,12.85],[14.84,15.52]][G][h] + 0.91, quant_z, G, h)
-        at([9.07,9.43,11.69][0], knots_a)
-        at([9.07,9.43,11.69][1], knots_b)
-        at([9.07,9.43,11.69][2], knots_c)
-        for m in range(MT):
-            split = m < 2
-            if split:
-                fronts = [17.73 + -1.98 * m, 22.12 + 3.8 * m]
-            else:
-                fronts = [26.82 + 2.12 * (m - 2)] * 2
-            for G in range(2):
-                at(fronts[G] - 0.82, stage2, m, G)
-            for G in range(2):
-                at(fronts[G], whole, m, G)
-            for G in range(2):
-                at(fronts[G] + 0.01, rest, m, G)
-            if split:
-                at(fronts[0] + 2.42, waves, m, 0, 2)
-                at(fronts[1] + 2.42, waves, m, 1, 2)
-            else:
-                at(fronts[1] + 2.42, waves, m, 0, 1)
-            last = max(fronts)
-            on_vector = m in [0, 1, 2, 3, 4, 5, 6, 7]
-            at(last + 5.08, terms, m, 2 if split else 1, nc.vector if on_vector else nc.gpsimd)
-            for G in range(2):
-                at(last + 6.53, turn_y, m, G)
-            for G in range(2):
-                at(last + 7.66, empty_y, m, G, (m, G) in [(3, 1), (4, 0), (6, 0), (6, 1), (1, 1), (2, 1), (0, 0), (3, 0), (5, 1), (7, 0), (0, 1), (7, 1)])
-            if m % 2:
-                for G in range(2):
-                    at(last + 7.66, store_rows, m // 2, G)
-            for G in range(2):
-                at(last + 9.78, lay_y, m, G)
-            for G in range(2):
-                at(last + 9.78 + 0.01, quant_y, m, G)
-            if m % 2:
-                for G in range(2):
-                    at(last + 9.78 + 0.02, store_words, m // 2, G)
+        load_scales(nc.sync, a_s, a_scales)
         with tc.manual_schedule():
-            for slot, tie, step, args in sorted(plan):
-                step(*args)
+            turn_x(0, 0, 0)
+            order_w(0)
+            turn_x(0, 0, 1)
+            knots_a()
+            turn_x(0, 1, 1)
+            turn_x(0, 1, 0)
+            knots_t()
+            copy_x(0, 0, 0, False)
+            copy_x(0, 0, 1, False)
+            copy_x(0, 1, 1, False)
+            copy_x(0, 1, 0, False)
+            quant_x(0, 0, 1)
+            quant_x(0, 0, 0)
+            knots_d()
+            order_w(1)
+            quant_x(0, 1, 1)
+            quant_x(0, 1, 0)
+            turn_x(1, 0, 0)
+            turn_x(1, 0, 1)
+            turn_x(1, 1, 1)
+            turn_x(1, 1, 0)
+            stage1(0, 0, 1, 0, 2)
+            stage1(0, 0, 3, 0, 2)
+            stage1(0, 0, 0, 0, 2)
+            stage1(0, 0, 2, 0, 2)
+            knots_b()
+            copy_x(1, 0, 0, False)
+            copy_x(1, 0, 1, False)
+            knots_g()
+            copy_x(1, 1, 1, False)
+            copy_x(1, 1, 0, False)
+            squash(0, 0, 1, 0, 2)
+            squash(0, 0, 3, 0, 2)
+            squash(0, 0, 0, 0, 2)
+            squash(0, 0, 2, 0, 2)
+            stage1(0, 1, 3, 0, 2)
+            stage1(0, 1, 2, 0, 2)
+            stage1(0, 0, 1, 1, 2)
+            stage1(0, 1, 0, 1, 2)
+            squash(0, 1, 3, 0, 2)
+            squash(0, 1, 2, 0, 2)
+            squash(0, 0, 1, 1, 2)
+            squash(0, 1, 0, 1, 2)
+            stage1(0, 1, 0, 0, 2)
+            stage1(0, 0, 3, 1, 2)
+            stage1(0, 1, 1, 0, 2)
+            stage1(0, 0, 2, 1, 2)
+            squash(0, 1, 0, 0, 2)
+            squash(0, 0, 3, 1, 2)
+            squash(0, 1, 1, 0, 2)
+            squash(0, 0, 2, 1, 2)
+            knots_c()
+            quant_x(1, 0, 0)
+            quant_x(1, 1, 1)
+            gain(0, 0, 0, 2, False)
+            quant_x(1, 1, 0)
+            quant_x(1, 0, 1)
+            gain(0, 1, 0, 2, False)
+            stage1(0, 1, 3, 1, 2)
+            stage1(0, 1, 1, 1, 2)
+            stage1(0, 1, 2, 1, 2)
+            stage1(0, 0, 0, 1, 2)
+            squash(0, 1, 3, 1, 2)
+            squash(0, 1, 1, 1, 2)
+            squash(0, 1, 2, 1, 2)
+            squash(0, 0, 0, 1, 2)
+            gain(0, 1, 1, 2, False)
+            gain(0, 0, 1, 2, False)
+            quant_z(0, 1)
+            quant_z(0, 0)
+            stage1(1, 0, 2, 0, 1)
+            stage1(1, 0, 1, 0, 1)
+            stage1(1, 0, 3, 0, 1)
+            stage1(1, 0, 0, 0, 1)
+            squash(1, 0, 2, 0, 1)
+            squash(1, 0, 1, 0, 1)
+            squash(1, 0, 3, 0, 1)
+            squash(1, 0, 0, 0, 1)
+            gain(1, 0, 0, 1, False)
+            stage1(1, 1, 3, 0, 1)
+            stage1(1, 1, 1, 0, 1)
+            stage1(1, 1, 0, 0, 1)
+            stage1(1, 1, 2, 0, 1)
+            squash(1, 1, 1, 0, 1)
+            squash(1, 1, 0, 0, 1)
+            squash(1, 1, 3, 0, 1)
+            scale_z(1, 1, 1)
+            squash(1, 1, 2, 0, 1)
+            scale_z(1, 1, 0)
+            scale_z(1, 1, 2)
+            scale_z(1, 1, 3)
+            stage2(1, 0)
+            stage2(2, 0)
+            stage2(0, 0)
+            stage2(3, 0)
+            whole(1, 0)
+            whole(2, 0)
+            rest(1, 0)
+            rest(2, 0)
+            quant_z(1, 0)
+            gain(1, 1, 0, 1, True)
+            whole(0, 0)
+            quant_z(1, 1)
+            rest(0, 0)
+            stage2(0, 1)
+            stage2(1, 1)
+            waves(1, 0, 2)
+            waves(2, 0, 2)
+            waves(0, 0, 2)
+            whole(3, 0)
+            whole(0, 1)
+            rest(0, 1)
+            whole(1, 1)
+            rest(1, 1)
+            rest(3, 0)
+            stage2(3, 1)
+            stage2(2, 1)
+            stage2(4, 0)
+            stage2(4, 1)
+            whole(2, 1)
+            whole(3, 1)
+            rest(2, 1)
+            waves(0, 1, 2)
+            waves(1, 1, 2)
+            waves(2, 1, 2)
+            terms(0, 2, nc.vector)
+            whole(4, 0)
+            rest(3, 1)
+            terms(1, 2, nc.vector)
+            rest(4, 0)
+            whole(4, 1)
+            rest(4, 1)
+            terms(2, 2, nc.vector)
+            stage2(7, 1)
+            turn_y(0, 0)
+            turn_y(0, 1)
+            stage2(5, 1)
+            turn_y(1, 1)
+            stage2(5, 0)
+            stage2(6, 0)
+            turn_y(2, 0)
+            empty_y(0, 0, True)
+            waves(3, 0, 1)
+            empty_y(0, 1, True)
+            empty_y(1, 1, True)
+            waves(4, 0, 1)
+            empty_y(2, 0, True)
+            whole(5, 0)
+            terms(3, 1, nc.vector)
+            whole(6, 0)
+            rest(5, 0)
+            whole(5, 1)
+            lay_y(1, 1)
+            rest(5, 1)
+            lay_y(0, 0)
+            turn_y(3, 1)
+            stage2(7, 0)
+            stage2(6, 1)
+            turn_y(1, 0)
+            turn_y(2, 1)
+            turn_y(3, 0)
+            empty_y(3, 1, True)
+            waves(5, 0, 1)
+            empty_y(2, 1, True)
+            empty_y(1, 0, True)
+            whole(7, 0)
+            lay_y(2, 0)
+            quant_y(1, 1)
+            lay_y(0, 1)
+            lay_y(3, 1)
+            whole(7, 1)
+            whole(6, 1)
+            quant_y(3, 1)
+            rest(7, 1)
+            quant_y(0, 0)
+            rest(6, 1)
+            terms(4, 1, nc.vector)
+            rest(6, 0)
+            terms(5, 1, nc.vector)
+            rest(7, 0)
+            quant_y(0, 1)
+            lay_y(2, 1)
+            quant_y(2, 1)
+            empty_y(3, 0, True)
+            waves(6, 0, 1)
+            turn_y(4, 1)
+            turn_y(5, 1)
+            turn_y(5, 0)
+            turn_y(4, 0)
+            quant_y(2, 0)
+            lay_y(3, 0)
+            empty_y(5, 1, False)
+            lay_y(1, 0)
+            empty_y(4, 1, False)
+            quant_y(3, 0)
+            quant_y(1, 0)
+            lay_y(4, 1)
+            terms(6, 1, nc.vector)
+            waves(7, 0, 1)
+            empty_y(5, 0, True)
+            empty_y(4, 0, True)
+            store_rows(0, 1)
+            store_rows(0, 0)
+            store_rows(1, 1)
+            store_words(1, 1)
+            store_rows(1, 0)
+            store_rows(2, 1)
+            store_words(1, 0)
+            store_words(0, 0)
+            store_words(0, 1)
+            quant_y(4, 1)
+            lay_y(5, 1)
+            quant_y(5, 1)
+            terms(7, 1, nc.vector)
+            turn_y(6, 1)
+            turn_y(6, 0)
+            turn_y(7, 0)
+            turn_y(7, 1)
+            empty_y(6, 0, True)
+            empty_y(7, 0, True)
+            empty_y(7, 1, True)
+            lay_y(5, 0)
+            lay_y(4, 0)
+            quant_y(5, 0)
+            quant_y(4, 0)
+            empty_y(6, 1, False)
+            lay_y(6, 0)
+            lay_y(6, 1)
+            lay_y(7, 0)
+            quant_y(6, 0)
+            lay_y(7, 1)
+            quant_y(7, 0)
+            quant_y(6, 1)
+            quant_y(7, 1)
+            store_words(2, 1)
+            store_rows(2, 0)
+            store_words(2, 0)
+            store_rows(3, 0)
+            store_rows(3, 1)
+            store_words(3, 1)
+            store_words(3, 0)
 
         for Q in range(4):
             nc.sync.dma_start(

@@ -19,8 +19,8 @@ N, F, D, M = 1024, 1024, 1024, 1024
 FLOPS = 2 * N * F * D + 2 * N * D * M
 HALF = 512
 MT = M // P
+ON_TENSOR = (1, 3, 5)
 TURN_SPLIT = 11.0
-ON_TENSOR = (2, 4, 5, 3)
 
 
 def tile_lejepasigregrandomknotslicegrad_x2_kernel(
@@ -76,9 +76,10 @@ def tile_lejepasigregrandomknotslicegrad_x2_kernel(
 
         x_in = x.rearrange("(G p t) f -> G p t f", G=2, t=4)
 
-        def load_x(G, first, count):
-            slots = slice(first, first + count)
-            nc.sync.dma_start(out=x_raw[G][:, slots, :], in_=x_in[G][:, slots, :])
+        def load_x(G, j, gk, count):
+            slots = slice(2 * j, 2 * j + 2)
+            cols = slice(512 * gk, 512 * (gk + count))
+            nc.sync.dma_start(out=x_raw[G][:, slots, cols], in_=x_in[G][:, slots, cols])
 
         def order_w(h):
             for gk in range(2):
@@ -114,12 +115,12 @@ def tile_lejepasigregrandomknotslicegrad_x2_kernel(
             else:
                 nc.scalar.copy(out=dst, in_=src)
 
-        def quant_x(G, j, gk):
-            cols = slice(256 * j, 256 * j + 256)
+        def quant_x(G, j, count, gk):
+            cols = slice(256 * j, 256 * (j + count))
             nc.vector.quantize_mx(
                 out=x_q[G][gk][:, cols].bitcast(E4M3),
                 scales=x_s[G][gk][:, cols],
-                in_=x_bf[G][gk][:, 1024 * j : 1024 * j + 1024],
+                in_=x_bf[G][gk][:, 1024 * j : 1024 * (j + count)],
             )
 
         z_q = [[keep.tile([P, HALF], U32, name="z_q%d%d" % (G, h), align_bytes=64) for h in range(2)] for G in range(2)]
@@ -276,20 +277,21 @@ def tile_lejepasigregrandomknotslicegrad_x2_kernel(
 
         diag = {}
 
-        def terms(m, parts, eng):
+        def terms(m, parts, pieces):
             if parts == 2:
                 nc.gpsimd.tensor_tensor(out=sums[m][:, 0, :], in0=sums[m][:, 0, :], in1=sums[m][:, 1, :], op=ALU.add)
             ab = work.tile([P, 3], F32, tag="ab", bufs=3, name="ab")
             nc.gpsimd.tensor_scalar(out=ab[:, 0:2], in0=co_a[:, m, :], scalar1=sums[m][:, 0, 0:1], scalar2=0.0, op0=ALU.mult, op1=ALU.add)
             nc.gpsimd.tensor_scalar(out=ab[:, 2:3], in0=sums[m][:, 0, 1:2], scalar1=co_b[:, m : m + 1], scalar2=b0[:, m : m + 1], op0=ALU.mult, op1=ALU.add)
-            for G in range(2):
-                cols = slice(HALF * G, HALF * G + HALF)
-                eng.tensor_scalar(out=sq_h[m][:, cols], in0=sq_h[m][:, cols], scalar1=ab[:, 1:2], scalar2=ab[:, 0:1], op0=ALU.mult, op1=ALU.add)
+            width = N // pieces
+            for first in range(0, N, width):
+                cols = slice(first, first + width)
+                nc.vector.tensor_scalar(out=sq_h[m][:, cols], in0=sq_h[m][:, cols], scalar1=ab[:, 1:2], scalar2=ab[:, 0:1], op0=ALU.mult, op1=ALU.add)
                 if m not in ON_TENSOR:
-                    eng.tensor_scalar(out=sin_u[m][:, cols], in0=sin_u[m][:, cols], scalar1=ab[:, 2:3], scalar2=0.0, op0=ALU.mult, op1=ALU.add)
+                    nc.vector.tensor_scalar(out=sin_u[m][:, cols], in0=sin_u[m][:, cols], scalar1=ab[:, 2:3], scalar2=0.0, op0=ALU.mult, op1=ALU.add)
             if m in ON_TENSOR:
-                diag[m] = work.tile([P, P], F32, tag="diag", bufs=3, name="diag")
-                eng.tensor_scalar(out=diag[m][:], in0=ident[:], scalar1=ab[:, 2:3], scalar2=None, op0=ALU.mult)
+                diag[m] = work.tile([P, P], F32, tag="diag", bufs=2, name="diag")
+                nc.vector.tensor_scalar(out=diag[m][:], in0=ident[:], scalar1=ab[:, 2:3], scalar2=None, op0=ALU.mult)
 
         def turn_y(m, G):
             yb[m, G] = psum.tile([P, 4, P], F32, tag="yb", bufs=4, name="yb")
@@ -302,293 +304,262 @@ def tile_lejepasigregrandomknotslicegrad_x2_kernel(
                     nc.tensor.matmul(yb[m, G][:, t, :], lhsT=sin_u[m][:, cols], rhs=ident[:], is_transpose=True, start=False, stop=True)
 
         def empty_y(m, G, on_scalar):
-            if (m // 2, G) not in r:
-                r[m // 2, G] = work.tile([P, 4, 2 * P], F32, tag="r%d" % G, bufs=3, name="r%d" % G)
-            dst = r[m // 2, G][:, :, P * (m % 2) : P * (m % 2) + P]
+            if m not in r:
+                r[m] = work.tile([P, 2, 4, P], F32, tag="r", bufs=5, name="r")
             if on_scalar:
-                nc.scalar.copy(out=dst, in_=yb[m, G][:])
+                nc.scalar.copy(out=r[m][:, G], in_=yb[m, G][:])
             else:
-                nc.vector.tensor_copy(out=dst, in_=yb[m, G][:])
+                nc.vector.tensor_copy(out=r[m][:, G], in_=yb[m, G][:])
+            nc.sync.dma_start(out=out_rows[G][:, :, P * m : P * m + P], in_=r[m][:, G])
 
-        def store_rows(b, G):
-            nc.sync.dma_start(out=out_rows[G][:, :, 256 * b : 256 * b + 256], in_=r[b, G][:])
-
-        def lay_y(m, G):
-            y_bf[m, G] = work.tile([P, P, 4], BF16, tag="y_bf", bufs=4, name="y_bf", align_bytes=64)
+        def lay_y(m, G, count):
+            if m not in y_bf:
+                y_bf[m] = work.tile([P, 2, P, 4], BF16, tag="y_bf", bufs=3, name="y_bf", align_bytes=64)
             nc.vector.tensor_copy(
-                out=y_bf[m, G][:].rearrange("p (b i) t -> p b t i", i=4),
-                in_=r[m // 2, G][:, :, P * (m % 2) : P * (m % 2) + P].rearrange("p t (b i) -> p b t i", i=4),
+                out=y_bf[m][:, G : G + count].rearrange("p g (b i) t -> p g b t i", i=4),
+                in_=r[m][:, G : G + count].rearrange("p g t (b i) -> p g b t i", i=4),
             )
 
-        def quant_y(m, G):
-            if (m // 2, G) not in y_q:
-                y_q[m // 2, G] = work.tile([P, 2 * P], U32, tag="y_q%d" % G, bufs=2, name="y_q%d" % G, align_bytes=64)
-            nc.vector.quantize_mx(
-                out=y_q[m // 2, G][:, P * (m % 2) : P * (m % 2) + P].bitcast(E4M3),
-                scales=y_s[:, G, P * m : P * m + P],
-                in_=y_bf[m, G][:].rearrange("p m t -> p (m t)"),
+        def quant_y(m):
+            y_q[m] = work.tile([P, 2, P], U32, tag="y_q", bufs=4, name="y_q", align_bytes=64)
+            for G in range(2):
+                nc.vector.quantize_mx(
+                    out=y_q[m][:, G].bitcast(E4M3),
+                    scales=y_s[:, G, P * m : P * m + P],
+                    in_=y_bf[m][:, G].rearrange("p m t -> p (m t)"),
+                )
+            nc.sync.dma_start(
+                out=out_1.rearrange("g p m t -> p g (m t)")[:, :, 4 * P * m : 4 * P * m + 4 * P].bitcast(I32), in_=y_q[m][:].bitcast(I32)
             )
 
-        def store_words(b, G):
-            nc.sync.dma_start(out=out_words[G][:, 1024 * b : 1024 * b + 1024].bitcast(I32), in_=y_q[b, G][:].bitcast(I32))
+        def store_scales(first, count):
+            cols = slice(P * first, P * (first + count))
+            for Q in range(4):
+                nc.sync.dma_start(
+                    out=out_2[:, 4 * Q : 4 * Q + 4, cols].rearrange("g r m -> r g m").bitcast(I32),
+                    in_=y_s[32 * Q : 32 * Q + 4, :, cols].bitcast(I32),
+                )
 
-        load_scales(nc.sync, w_sraw, w_scales)
         nc.gpsimd.dma_start(out=c_col[:], in_=c.rearrange("(g p t) -> p g t", g=2, t=4))
         nc.gpsimd.dma_start(out=g_col[:], in_=g.rearrange("(g p t) -> p g t", g=2, t=4))
         nc.gpsimd.dma_start(out=s_row[:], in_=s.rearrange("(j p) -> j p", p=P))
-        load_x(0, 0, 2)
+        load_x(0, 0, 0, 2)
         load_w(0)
-        load_x(0, 2, 2)
+        load_scales(nc.sync, w_sraw, w_scales)
+        load_x(0, 1, 0, 2)
         load_w(1)
-        load_x(1, 0, 2)
-        load_x(1, 2, 2)
+        load_x(1, 0, 0, 2)
+        load_x(1, 1, 0, 2)
         nc.sync.dma_start(out=a_raw[:].bitcast(I32), in_=a_in.bitcast(I32))
         load_scales(nc.sync, a_s, a_scales)
         with tc.manual_schedule():
-            turn_x(0, 0, 0)
-            order_w(0)
+            knots_g()
             turn_x(0, 0, 1)
+            order_w(0)
+            turn_x(0, 0, 0)
+            copy_x(0, 0, 1, False)
+            copy_x(0, 0, 0, False)
+            quant_x(0, 0, 1, 0)
+            quant_x(0, 0, 1, 1)
+            order_w(1)
             knots_a()
             turn_x(0, 1, 1)
             turn_x(0, 1, 0)
-            knots_t()
-            copy_x(0, 0, 0, False)
-            copy_x(0, 0, 1, False)
-            copy_x(0, 1, 1, False)
-            copy_x(0, 1, 0, False)
-            quant_x(0, 0, 1)
-            quant_x(0, 0, 0)
-            knots_d()
-            order_w(1)
-            quant_x(0, 1, 1)
-            quant_x(0, 1, 0)
-            turn_x(1, 0, 0)
-            turn_x(1, 0, 1)
-            turn_x(1, 1, 1)
-            turn_x(1, 1, 0)
-            stage1(0, 0, 1, 0, 2)
             stage1(0, 0, 3, 0, 2)
             stage1(0, 0, 0, 0, 2)
             stage1(0, 0, 2, 0, 2)
-            knots_b()
-            copy_x(1, 0, 0, False)
-            copy_x(1, 0, 1, False)
-            knots_g()
-            copy_x(1, 1, 1, False)
-            copy_x(1, 1, 0, False)
-            squash(0, 0, 1, 0, 2)
+            stage1(0, 0, 1, 0, 2)
+            copy_x(0, 1, 0, False)
             squash(0, 0, 3, 0, 2)
+            copy_x(0, 1, 1, False)
             squash(0, 0, 0, 0, 2)
             squash(0, 0, 2, 0, 2)
+            squash(0, 0, 1, 0, 2)
+            turn_x(1, 0, 1)
+            turn_x(1, 0, 0)
+            knots_t()
+            turn_x(1, 1, 1)
+            turn_x(1, 1, 0)
+            gain(0, 0, 0, 2, False)
+            knots_d()
+            quant_x(0, 1, 1, 0)
+            quant_x(0, 1, 1, 1)
             stage1(0, 1, 3, 0, 2)
             stage1(0, 1, 2, 0, 2)
-            stage1(0, 0, 1, 1, 2)
-            stage1(0, 1, 0, 1, 2)
+            stage1(0, 1, 0, 0, 2)
+            stage1(0, 1, 1, 0, 2)
+            copy_x(1, 0, 1, False)
+            copy_x(1, 0, 0, False)
+            copy_x(1, 1, 1, False)
+            copy_x(1, 1, 0, False)
             squash(0, 1, 3, 0, 2)
             squash(0, 1, 2, 0, 2)
-            squash(0, 0, 1, 1, 2)
-            squash(0, 1, 0, 1, 2)
-            stage1(0, 1, 0, 0, 2)
-            stage1(0, 0, 3, 1, 2)
-            stage1(0, 1, 1, 0, 2)
-            stage1(0, 0, 2, 1, 2)
             squash(0, 1, 0, 0, 2)
-            squash(0, 0, 3, 1, 2)
             squash(0, 1, 1, 0, 2)
-            squash(0, 0, 2, 1, 2)
-            knots_c()
-            quant_x(1, 0, 0)
-            quant_x(1, 1, 1)
-            gain(0, 0, 0, 2, False)
-            quant_x(1, 1, 0)
-            quant_x(1, 0, 1)
-            gain(0, 1, 0, 2, False)
+            stage1(0, 0, 3, 1, 2)
+            stage1(0, 1, 2, 1, 2)
+            stage1(0, 0, 1, 1, 2)
+            stage1(0, 0, 0, 1, 2)
+            squash(0, 0, 3, 1, 2)
+            knots_b()
+            squash(0, 1, 2, 1, 2)
+            squash(0, 0, 1, 1, 2)
+            squash(0, 0, 0, 1, 2)
+            stage1(0, 0, 2, 1, 2)
             stage1(0, 1, 3, 1, 2)
             stage1(0, 1, 1, 1, 2)
-            stage1(0, 1, 2, 1, 2)
-            stage1(0, 0, 0, 1, 2)
+            stage1(0, 1, 0, 1, 2)
+            squash(0, 0, 2, 1, 2)
             squash(0, 1, 3, 1, 2)
+            squash(0, 1, 0, 1, 2)
             squash(0, 1, 1, 1, 2)
-            squash(0, 1, 2, 1, 2)
-            squash(0, 0, 0, 1, 2)
-            gain(0, 1, 1, 2, False)
+            quant_x(1, 0, 2, 1)
+            quant_x(1, 0, 2, 0)
+            gain(0, 1, 0, 2, False)
             gain(0, 0, 1, 2, False)
-            quant_z(0, 1)
+            knots_c()
+            gain(0, 1, 1, 2, False)
             quant_z(0, 0)
-            stage1(1, 0, 2, 0, 1)
-            stage1(1, 0, 1, 0, 1)
-            stage1(1, 0, 3, 0, 1)
+            quant_z(0, 1)
             stage1(1, 0, 0, 0, 1)
-            squash(1, 0, 2, 0, 1)
-            squash(1, 0, 1, 0, 1)
-            squash(1, 0, 3, 0, 1)
-            squash(1, 0, 0, 0, 1)
-            gain(1, 0, 0, 1, False)
             stage1(1, 1, 3, 0, 1)
-            stage1(1, 1, 1, 0, 1)
+            stage1(1, 0, 1, 0, 1)
+            stage1(1, 0, 2, 0, 1)
+            squash(1, 0, 0, 0, 1)
+            squash(1, 1, 3, 0, 1)
+            squash(1, 0, 1, 0, 1)
+            squash(1, 0, 2, 0, 1)
+            stage1(1, 0, 3, 0, 1)
             stage1(1, 1, 0, 0, 1)
             stage1(1, 1, 2, 0, 1)
-            squash(1, 1, 1, 0, 1)
+            stage1(1, 1, 1, 0, 1)
+            squash(1, 0, 3, 0, 1)
             squash(1, 1, 0, 0, 1)
-            squash(1, 1, 3, 0, 1)
-            scale_z(1, 1, 1)
             squash(1, 1, 2, 0, 1)
-            scale_z(1, 1, 0)
             scale_z(1, 1, 2)
+            squash(1, 1, 1, 0, 1)
+            scale_z(1, 1, 1)
+            scale_z(1, 1, 0)
             scale_z(1, 1, 3)
-            stage2(1, 0)
-            stage2(2, 0)
             stage2(0, 0)
             stage2(3, 0)
-            whole(1, 0)
-            whole(2, 0)
-            rest(1, 0)
-            rest(2, 0)
-            quant_z(1, 0)
-            gain(1, 1, 0, 1, True)
+            stage2(1, 0)
+            stage2(2, 0)
+            gain(1, 0, 0, 1, False)
             whole(0, 0)
-            quant_z(1, 1)
+            quant_z(1, 0)
             rest(0, 0)
-            stage2(0, 1)
+            whole(1, 0)
+            gain(1, 1, 0, 1, True)
+            rest(1, 0)
+            whole(2, 0)
+            quant_z(1, 1)
+            rest(2, 0)
             stage2(1, 1)
-            waves(1, 0, 2)
-            waves(2, 0, 2)
-            waves(0, 0, 2)
+            stage2(2, 1)
             whole(3, 0)
-            whole(0, 1)
-            rest(0, 1)
             whole(1, 1)
             rest(1, 1)
-            rest(3, 0)
+            stage2(0, 1)
             stage2(3, 1)
-            stage2(2, 1)
+            waves(0, 0, 2)
+            waves(1, 0, 2)
+            waves(2, 0, 2)
+            waves(1, 1, 2)
+            whole(0, 1)
+            whole(2, 1)
+            rest(0, 1)
+            whole(3, 1)
+            rest(3, 0)
+            rest(3, 1)
+            rest(2, 1)
+            terms(1, 2, 1)
+            stage2(6, 1)
             stage2(4, 0)
             stage2(4, 1)
-            whole(2, 1)
-            whole(3, 1)
-            rest(2, 1)
-            waves(0, 1, 2)
-            waves(1, 1, 2)
-            waves(2, 1, 2)
-            terms(0, 2, nc.vector)
-            whole(4, 0)
-            rest(3, 1)
-            terms(1, 2, nc.vector)
-            rest(4, 0)
-            whole(4, 1)
-            rest(4, 1)
-            terms(2, 2, nc.vector)
-            stage2(7, 1)
-            turn_y(0, 0)
-            turn_y(0, 1)
-            stage2(5, 1)
-            turn_y(1, 1)
-            stage2(5, 0)
-            stage2(6, 0)
-            turn_y(2, 0)
-            empty_y(0, 0, True)
-            waves(3, 0, 1)
-            empty_y(0, 1, True)
-            empty_y(1, 1, True)
-            waves(4, 0, 1)
-            empty_y(2, 0, True)
-            whole(5, 0)
-            terms(3, 1, nc.vector)
-            whole(6, 0)
-            rest(5, 0)
-            whole(5, 1)
-            lay_y(1, 1)
-            rest(5, 1)
-            lay_y(0, 0)
-            turn_y(3, 1)
             stage2(7, 0)
-            stage2(6, 1)
+            turn_y(1, 1)
             turn_y(1, 0)
-            turn_y(2, 1)
-            turn_y(3, 0)
-            empty_y(3, 1, True)
-            waves(5, 0, 1)
-            empty_y(2, 1, True)
+            waves(0, 1, 2)
+            waves(3, 0, 1)
+            waves(2, 1, 2)
+            empty_y(1, 1, True)
             empty_y(1, 0, True)
-            whole(7, 0)
-            lay_y(2, 0)
-            quant_y(1, 1)
-            lay_y(0, 1)
-            lay_y(3, 1)
-            whole(7, 1)
+            whole(4, 1)
+            whole(4, 0)
+            rest(4, 1)
             whole(6, 1)
-            quant_y(3, 1)
-            rest(7, 1)
-            quant_y(0, 0)
+            terms(0, 2, 1)
+            whole(7, 0)
+            rest(4, 0)
+            terms(3, 1, 1)
             rest(6, 1)
-            terms(4, 1, nc.vector)
-            rest(6, 0)
-            terms(5, 1, nc.vector)
             rest(7, 0)
-            quant_y(0, 1)
-            lay_y(2, 1)
-            quant_y(2, 1)
+            stage2(5, 0)
+            stage2(5, 1)
+            stage2(6, 0)
+            turn_y(0, 1)
+            turn_y(0, 0)
+            turn_y(3, 0)
+            turn_y(3, 1)
+            waves(4, 0, 1)
+            whole(5, 0)
+            whole(5, 1)
+            whole(6, 0)
+            terms(2, 2, 1)
+            lay_y(1, 0, 2)
+            rest(6, 0)
+            rest(5, 0)
+            rest(5, 1)
+            empty_y(0, 0, True)
+            empty_y(0, 1, True)
+            terms(4, 1, 1)
+            lay_y(0, 0, 2)
+            quant_y(1)
             empty_y(3, 0, True)
-            waves(6, 0, 1)
-            turn_y(4, 1)
-            turn_y(5, 1)
-            turn_y(5, 0)
+            empty_y(3, 1, False)
+            waves(5, 0, 1)
             turn_y(4, 0)
-            quant_y(2, 0)
-            lay_y(3, 0)
-            empty_y(5, 1, False)
-            lay_y(1, 0)
+            turn_y(4, 1)
+            turn_y(2, 1)
+            stage2(7, 1)
+            turn_y(2, 0)
+            empty_y(4, 0, False)
+            lay_y(3, 0, 2)
+            quant_y(0)
             empty_y(4, 1, False)
-            quant_y(3, 0)
-            quant_y(1, 0)
-            lay_y(4, 1)
-            terms(6, 1, nc.vector)
-            waves(7, 0, 1)
-            empty_y(5, 0, True)
-            empty_y(4, 0, True)
-            store_rows(0, 1)
-            store_rows(0, 0)
-            store_rows(1, 1)
-            store_words(1, 1)
-            store_rows(1, 0)
-            store_rows(2, 1)
-            store_words(1, 0)
-            store_words(0, 0)
-            store_words(0, 1)
-            quant_y(4, 1)
-            lay_y(5, 1)
-            quant_y(5, 1)
-            terms(7, 1, nc.vector)
+            empty_y(2, 1, True)
+            quant_y(3)
+            terms(5, 1, 1)
+            whole(7, 1)
+            lay_y(4, 0, 2)
+            empty_y(2, 0, False)
+            waves(6, 0, 1)
+            rest(7, 1)
+            lay_y(2, 0, 2)
+            quant_y(4)
+            quant_y(2)
+            terms(6, 1, 1)
+            turn_y(5, 0)
+            turn_y(5, 1)
             turn_y(6, 1)
             turn_y(6, 0)
+            empty_y(5, 0, True)
+            waves(7, 0, 1)
+            empty_y(5, 1, False)
+            lay_y(5, 0, 2)
+            empty_y(6, 1, False)
+            quant_y(5)
+            store_scales(0, 6)
+            empty_y(6, 0, True)
+            terms(7, 1, 2)
             turn_y(7, 0)
             turn_y(7, 1)
-            empty_y(6, 0, True)
+            lay_y(6, 0, 2)
             empty_y(7, 0, True)
-            empty_y(7, 1, True)
-            lay_y(5, 0)
-            lay_y(4, 0)
-            quant_y(5, 0)
-            quant_y(4, 0)
-            empty_y(6, 1, False)
-            lay_y(6, 0)
-            lay_y(6, 1)
-            lay_y(7, 0)
-            quant_y(6, 0)
-            lay_y(7, 1)
-            quant_y(7, 0)
-            quant_y(6, 1)
-            quant_y(7, 1)
-            store_words(2, 1)
-            store_rows(2, 0)
-            store_words(2, 0)
-            store_rows(3, 0)
-            store_rows(3, 1)
-            store_words(3, 1)
-            store_words(3, 0)
-
-        for Q in range(4):
-            nc.sync.dma_start(
-                out=out_2[:, 4 * Q : 4 * Q + 4, :].rearrange("g r m -> r g m").bitcast(I32),
-                in_=y_s[32 * Q : 32 * Q + 4, :, :].bitcast(I32),
-            )
+            quant_y(6)
+            empty_y(7, 1, False)
+            lay_y(7, 0, 1)
+            lay_y(7, 1, 1)
+            quant_y(7)
+            store_scales(6, 2)

from contextlib import ExitStack
import math

import concourse.mybir as mybir
from concourse.masks import make_identity

F32 = mybir.dt.float32
BF16 = mybir.dt.bfloat16
I32 = mybir.dt.int32
U32 = mybir.dt.uint32
U8 = mybir.dt.uint8
E4M3 = mybir.dt.float8_e4m3fn_x4
E2M1 = mybir.dt.float4_e2m1fn_x4
AF = mybir.ActivationFunctionType
ALU = mybir.AluOpType

P = 128
N, F, D, M = 1024, 1024, 1024, 1024
FLOPS = 2 * N * F * D + 2 * N * D * M
HALF = 512
MT = M // P
ON_TENSOR = (1, 3, 5)
TURN_SPLIT = 11.0


def tile_lejepasigregrandomknotslicegrad_x2_kernel(
    tc, x, w_words, w_scales, c, g, a_words, a_scales, s, out_0, out_1, out_2
):
    nc = tc.nc
    with ExitStack() as ctx:
        keep = ctx.enter_context(tc.tile_pool(name="keep", bufs=1))
        work = ctx.enter_context(tc.tile_pool(name="work", bufs=2))
        psum = ctx.enter_context(tc.psum_pool(name="psum", bufs=1))

        ident = keep.tile([P, P], F32, name="ident")
        zero = keep.tile([P, 1], F32, name="zero")
        silu0 = keep.tile([P, 1], F32, name="silu0")
        nc.vector.memset(zero[:], 0.0)
        nc.scalar.activation(out=silu0[:], in_=zero[:], func=AF.Silu)
        two_pi = keep.tile([P, 1], F32, name="two_pi")
        nc.vector.tensor_scalar(out=two_pi[:], in0=zero[:], scalar1=2.0 * math.pi / TURN_SPLIT, scalar2=TURN_SPLIT, op0=ALU.add, op1=ALU.mult)

        w_raw = keep.tile([P, 2, 2048], U8, name="w_raw", align_bytes=64)
        w_sraw = keep.tile([P, 2, 1024], U8, name="w_sraw", align_bytes=64)
        w_ord = keep.tile([P, 2, 2048], U8, name="w_ord", align_bytes=64)
        w_sord = keep.tile([P, 2, 1024], U8, name="w_sord", align_bytes=64)
        a_raw = keep.tile([P, 2, 2048], U8, name="a_raw", align_bytes=64)
        a_s = keep.tile([P, 2, 1024], U8, name="a_s", align_bytes=64)
        x_raw = [keep.tile([P, 4, F], BF16, name="x_raw%d" % G, align_bytes=64) for G in range(2)]
        c_col = keep.tile([P, 2, 4], BF16, name="c_col")
        g_f32 = keep.tile([P, 2, 4], F32, name="g_f32")
        g_col = keep.tile([P, 2, 4], BF16, name="g_col")
        s_row = keep.tile([8, P], BF16, name="s_row")
        s_pad = keep.tile([P, P], F32, name="s_pad")

        nc.vector.memset(w_sraw[:].rearrange("p g n -> p (g n)").bitcast(I32), 0)
        make_identity(nc, ident[:])
        nc.vector.memset(s_pad[:], 0.0)
        nc.vector.memset(a_s[:].rearrange("p g n -> p (g n)").bitcast(I32), 0)

        w_in = w_words.rearrange("g p n -> p g n")
        a_in = a_words.rearrange("g p n -> p g n")

        def load_w(h):
            nc.sync.dma_start(
                out=w_raw[:, :, 1024 * h : 1024 * h + 1024].bitcast(I32),
                in_=w_in[:, :, 1024 * h : 1024 * h + 1024].bitcast(I32),
            )

        def load_scales(queue, dst, src):
            for Q in range(4):
                queue.dma_start(
                    out=dst[32 * Q : 32 * Q + 4, :, :].bitcast(I32),
                    in_=src[:, 4 * Q : 4 * Q + 4, :].rearrange("g r n -> r g n").bitcast(I32),
                )

        x_in = x.rearrange("(G p t) f -> G p t f", G=2, t=4)

        def load_x(G, j, gk, count):
            slots = slice(2 * j, 2 * j + 2)
            cols = slice(512 * gk, 512 * (gk + count))
            nc.sync.dma_start(out=x_raw[G][:, slots, cols], in_=x_in[G][:, slots, cols])

        def order_w(h):
            for gk in range(2):
                nc.vector.tensor_copy(
                    out=w_ord[:, gk, 1024 * h : 1024 * h + 1024].rearrange("p (t m b) -> p t m b", t=4, b=2),
                    in_=w_raw[:, gk, 1024 * h : 1024 * h + 1024].rearrange("p (m t b) -> p t m b", t=4, b=2),
                )
            nc.vector.tensor_copy(
                out=w_sord[:, :, 512 * h : 512 * h + 512].rearrange("p g (t m) -> p g t m", t=4),
                in_=w_sraw[:, :, 512 * h : 512 * h + 512].rearrange("p g (m t) -> p g t m", t=4),
            )

        x_bf = [[keep.tile([P, 2048], BF16, name="x_bf%d%d" % (G, gk), align_bytes=64) for gk in range(2)] for G in range(2)]
        x_q = [[keep.tile([P, HALF], U32, name="x_q%d%d" % (G, gk), align_bytes=64) for gk in range(2)] for G in range(2)]
        x_s = [[keep.tile([P, HALF], U8, name="x_s%d%d" % (G, gk), align_bytes=64) for gk in range(2)] for G in range(2)]

        xt = {}

        def turn_x(G, j, gk):
            bank = psum.tile([P, 2, 2, P], F32, tag="yb", bufs=4, name="xt")
            words = x_raw[G][:].rearrange("p t f -> p (t f)").bitcast(F32)
            for i in range(2):
                for u in range(2):
                    first = 512 * (2 * j + i) + 256 * gk + u
                    nc.tensor.transpose(bank[:, i, u, :], words[:, first : first + 256 - u : 2], ident[:])
            xt[G, j, gk] = bank

        def copy_x(G, j, gk, on_vector):
            dst = x_bf[G][gk][:].bitcast(F32).rearrange("q (t r u) -> q t r u", t=4, u=2)[:, 2 * j : 2 * j + 2]
            src = xt[G, j, gk][:].rearrange("q i u r -> q i r u")
            if on_vector:
                nc.vector.tensor_copy(out=dst, in_=src)
            else:
                nc.scalar.copy(out=dst, in_=src)

        def quant_x(G, j, count, gk):
            cols = slice(256 * j, 256 * (j + count))
            nc.vector.quantize_mx(
                out=x_q[G][gk][:, cols].bitcast(E4M3),
                scales=x_s[G][gk][:, cols],
                in_=x_bf[G][gk][:, 1024 * j : 1024 * (j + count)],
            )

        z_q = [[keep.tile([P, HALF], U32, name="z_q%d%d" % (G, h), align_bytes=64) for h in range(2)] for G in range(2)]
        z_s = [[keep.tile([P, HALF], U8, name="z_s%d%d" % (G, h), align_bytes=64) for h in range(2)] for G in range(2)]
        th = {}
        zb = {}
        hb = {}

        def stage1(G, h, t, part, parts):
            hb[G, h, t, part] = psum.tile([P, HALF], F32, tag="mm", bufs=4, name="hb")
            width = HALF if parts == 1 else P
            for first in range(0, HALF // parts, width):
                cols = slice(HALF // parts * part + first, HALF // parts * part + first + width)
                for gk in range(2):
                    nc.tensor.matmul_mx(
                        out=hb[G, h, t, part][:, first : first + width],
                        lhsT=w_ord[:, gk, 1024 * h + 256 * t : 1024 * h + 256 * t + 256].bitcast(E2M1),
                        lhsT_scale=w_sord[:, gk, 512 * h + 128 * t : 512 * h + 128 * t + 128],
                        rhs=x_q[G][gk][:, cols].bitcast(E4M3),
                        rhs_scale=x_s[G][gk][:, cols],
                        start=(gk == 0),
                        stop=(gk == 1),
                    )

        def squash(G, h, t, part, parts):
            width = HALF // parts
            if (G, h) not in th:
                th[G, h] = work.tile([P, 4, HALF], F32, tag="th", bufs=3, name="th")
            nc.scalar.activation(
                out=th[G, h][:, t, width * part : width * part + width], in_=hb[G, h, t, part][:, 0:width], func=AF.Tanh, bias=c_col[:, h, t : t + 1]
            )

        zt = {}

        def scale_z(G, h, t):
            if (G, h) not in zt:
                zt[G, h] = work.tile([P, 4, HALF], BF16, tag="zt", bufs=1, name="zt")
            nc.scalar.activation(out=zt[G, h][:, t, :], in_=th[G, h][:, t, :], func=AF.Copy, scale=g_f32[:, h, t : t + 1])

        def gain(G, h, part, parts, scaled):
            if (G, h) not in zb:
                zb[G, h] = work.tile([P, HALF, 4], BF16, tag="zb", bufs=2, name="zb", align_bytes=64)
            width = HALF // parts
            cols = slice(width * part, width * part + width)
            dst = zb[G, h][:, cols, :].rearrange("p (b i) t -> p b t i", i=4)
            if scaled:
                nc.vector.tensor_copy(out=dst, in_=zt[G, h][:, :, cols].rearrange("p t (b i) -> p b t i", i=4))
            else:
                nc.vector.tensor_tensor(
                    out=dst,
                    in0=th[G, h][:, :, cols].rearrange("p t (b i) -> p b t i", i=4),
                    in1=g_col[:, h, :].unsqueeze(1).unsqueeze(3).to_broadcast([P, width // 4, 4, 4]),
                    op=ALU.mult,
                )

        def quant_z(G, h):
            nc.vector.quantize_mx(
                out=z_q[G][h][:].bitcast(E4M3), scales=z_s[G][h][:], in_=zb[G, h][:].rearrange("p n t -> p (n t)")
            )

        sc = keep.tile([P, MT], F32, name="sc")
        turns = keep.tile([P, MT], F32, name="turns")
        sq = keep.tile([P, MT], F32, name="sq")
        th_s = keep.tile([P, MT], F32, name="th_s")
        den = keep.tile([P, MT], F32, name="den")
        rec = keep.tile([P, MT], F32, name="rec")
        num = keep.tile([P, MT], F32, name="num")
        b0 = keep.tile([P, MT], F32, name="b0")
        co_a = keep.tile([P, MT, 2], F32, name="co_a")
        co_b = keep.tile([P, MT], F32, name="co_b")

        knot_bank = []

        def knots_a():
            nc.vector.tensor_copy(out=s_pad[0:8, :], in_=s_row[:])

        def knots_t():
            s_bank = psum.tile([P, P], F32, tag="mm", bufs=4, name="s_bank")
            nc.tensor.transpose(s_bank[:], s_pad[:], ident[:])
            knot_bank.append(s_bank)

        def knots_g():
            nc.gpsimd.tensor_copy(out=g_f32[:], in_=g_col[:])

        def knots_d():
            s_bank = knot_bank[0]
            nc.vector.tensor_copy(out=sc[:], in_=s_bank[:, 0:MT])
            nc.vector.tensor_scalar(out=turns[:], in0=sc[:], scalar1=1.0 / (2.0 * math.pi), scalar2=None, op0=ALU.mult)
            nc.gpsimd.tensor_tensor(out=sq[:], in0=sc[:], in1=sc[:], op=ALU.mult)
            nc.gpsimd.tensor_scalar(out=co_a[:, :, 0], in0=sc[:], scalar1=4.0 / N, scalar2=0.0, op0=ALU.mult, op1=ALU.add)
            nc.gpsimd.tensor_scalar(out=co_a[:, :, 1], in0=sc[:], scalar1=-8.0 / N, scalar2=0.0, op0=ALU.mult, op1=ALU.add)
            nc.gpsimd.tensor_scalar(out=co_b[:], in0=sc[:], scalar1=8.0 / N, scalar2=0.0, op0=ALU.mult, op1=ALU.add)

        def knots_b():
            nc.scalar.activation(out=th_s[:], in_=sq[:], func=AF.Tanh, scale=0.25, bias=silu0[:])
            nc.gpsimd.tensor_scalar(out=den[:], in0=th_s[:], scalar1=1.0, scalar2=0.0, op0=ALU.add, op1=ALU.add)
            nc.gpsimd.tensor_tensor(out=num[:], in0=th_s[:], in1=sc[:], op=ALU.mult)

        def knots_c():
            nc.vector.reciprocal(out=rec[:], in_=den[:])
            nc.vector.scalar_tensor_tensor(out=b0[:], in0=num[:], scalar=-8.0, in1=rec[:], op0=ALU.mult, op1=ALU.mult)

        y_s = keep.tile([P, 2, M], U8, name="y_s", align_bytes=64)
        out_rows = out_0.rearrange("(G p t) m -> G p t m", G=2, t=4)
        out_words = out_1.rearrange("G p m t -> G p (m t)")

        tb = {}
        k_t = {}
        f_t = {}
        sums = {}
        sin_u = {}
        sin_h = {}
        sq_h = {}
        yb = {}
        r = {}
        y_bf = {}
        y_q = {}

        def stage2(m, G):
            tb[m, G] = psum.tile([P, HALF], F32, tag="mm", bufs=4, name="tb")
            for h in range(2):
                nc.tensor.matmul_mx(
                    out=tb[m, G][:],
                    lhsT=a_raw[:, h, 256 * m : 256 * m + 256].bitcast(E2M1),
                    lhsT_scale=a_s[:, h, 128 * m : 128 * m + 128],
                    rhs=z_q[G][h][:].bitcast(E4M3),
                    rhs_scale=z_s[G][h][:],
                    start=(h == 0),
                    stop=(h == 1),
                )

        def whole(m, G):
            k_t[m, G] = work.tile([P, HALF], I32, tag="k_t", bufs=4, name="k_t")
            nc.vector.tensor_scalar(out=k_t[m, G][:], in0=tb[m, G][:], scalar1=turns[:, m : m + 1], scalar2=None, op0=ALU.mult)

        def rest(m, G):
            if m not in f_t:
                f_t[m] = work.tile([P, N], F32, tag="f_t", bufs=5, name="f_t")
            nc.vector.scalar_tensor_tensor(
                out=f_t[m][:, HALF * G : HALF * G + HALF], in0=tb[m, G][:], scalar=turns[:, m : m + 1], in1=k_t[m, G][:], op0=ALU.mult, op1=ALU.subtract
            )

        def waves(m, part, parts):
            width = N // parts
            cols = slice(width * part, width * part + width)
            if m not in sums:
                sums[m] = work.tile([P, 2, 2], F32, tag="sums", bufs=5, name="sums")
                sin_u[m] = work.tile([P, N], F32, tag="sin_u", bufs=6, name="sin_u")
                sq_h[m] = work.tile([P, N], F32, tag="sq_h", bufs=6, name="sq_h")
            sin_h = work.tile([P, N], F32, tag="sin_h", bufs=2, name="sin_h")
            nc.scalar.activation(out=sin_u[m][:, cols], in_=f_t[m][:, cols], func=AF.Sin, scale=two_pi[:], accum_out=sums[m][:, part, 0:1])
            nc.scalar.activation(out=sin_h[:, cols], in_=f_t[m][:, cols], func=AF.Sin, scale=math.pi)
            nc.scalar.activation(out=sq_h[m][:, cols], in_=sin_h[:, cols], func=AF.Square, accum_out=sums[m][:, part, 1:2])

        diag = {}

        def terms(m, parts, pieces):
            if parts == 2:
                nc.gpsimd.tensor_tensor(out=sums[m][:, 0, :], in0=sums[m][:, 0, :], in1=sums[m][:, 1, :], op=ALU.add)
            ab = work.tile([P, 3], F32, tag="ab", bufs=3, name="ab")
            nc.gpsimd.tensor_scalar(out=ab[:, 0:2], in0=co_a[:, m, :], scalar1=sums[m][:, 0, 0:1], scalar2=0.0, op0=ALU.mult, op1=ALU.add)
            nc.gpsimd.tensor_scalar(out=ab[:, 2:3], in0=sums[m][:, 0, 1:2], scalar1=co_b[:, m : m + 1], scalar2=b0[:, m : m + 1], op0=ALU.mult, op1=ALU.add)
            width = N // pieces
            for first in range(0, N, width):
                cols = slice(first, first + width)
                nc.vector.tensor_scalar(out=sq_h[m][:, cols], in0=sq_h[m][:, cols], scalar1=ab[:, 1:2], scalar2=ab[:, 0:1], op0=ALU.mult, op1=ALU.add)
                if m not in ON_TENSOR:
                    nc.vector.tensor_scalar(out=sin_u[m][:, cols], in0=sin_u[m][:, cols], scalar1=ab[:, 2:3], scalar2=0.0, op0=ALU.mult, op1=ALU.add)
            if m in ON_TENSOR:
                diag[m] = work.tile([P, P], F32, tag="diag", bufs=2, name="diag")
                nc.vector.tensor_scalar(out=diag[m][:], in0=ident[:], scalar1=ab[:, 2:3], scalar2=None, op0=ALU.mult)

        def turn_y(m, G):
            yb[m, G] = psum.tile([P, 4, P], F32, tag="yb", bufs=4, name="yb")
            for t in range(4):
                cols = slice(HALF * G + P * t, HALF * G + P * t + P)
                nc.tensor.matmul(yb[m, G][:, t, :], lhsT=sq_h[m][:, cols], rhs=ident[:], is_transpose=True, start=True, stop=False)
                if m in ON_TENSOR:
                    nc.tensor.matmul(yb[m, G][:, t, :], lhsT=sin_u[m][:, cols], rhs=diag[m][:], start=False, stop=True)
                else:
                    nc.tensor.matmul(yb[m, G][:, t, :], lhsT=sin_u[m][:, cols], rhs=ident[:], is_transpose=True, start=False, stop=True)

        def empty_y(m, G, on_scalar):
            if m not in r:
                r[m] = work.tile([P, 2, 4, P], F32, tag="r", bufs=5, name="r")
            if on_scalar:
                nc.scalar.copy(out=r[m][:, G], in_=yb[m, G][:])
            else:
                nc.vector.tensor_copy(out=r[m][:, G], in_=yb[m, G][:])
            nc.sync.dma_start(out=out_rows[G][:, :, P * m : P * m + P], in_=r[m][:, G])

        def lay_y(m, G, count):
            if m not in y_bf:
                y_bf[m] = work.tile([P, 2, P, 4], BF16, tag="y_bf", bufs=3, name="y_bf", align_bytes=64)
            nc.vector.tensor_copy(
                out=y_bf[m][:, G : G + count].rearrange("p g (b i) t -> p g b t i", i=4),
                in_=r[m][:, G : G + count].rearrange("p g t (b i) -> p g b t i", i=4),
            )

        def quant_y(m):
            y_q[m] = work.tile([P, 2, P], U32, tag="y_q", bufs=4, name="y_q", align_bytes=64)
            for G in range(2):
                nc.vector.quantize_mx(
                    out=y_q[m][:, G].bitcast(E4M3),
                    scales=y_s[:, G, P * m : P * m + P],
                    in_=y_bf[m][:, G].rearrange("p m t -> p (m t)"),
                )
            nc.sync.dma_start(
                out=out_1.rearrange("g p m t -> p g (m t)")[:, :, 4 * P * m : 4 * P * m + 4 * P].bitcast(I32), in_=y_q[m][:].bitcast(I32)
            )

        def store_scales(first, count):
            cols = slice(P * first, P * (first + count))
            for Q in range(4):
                nc.sync.dma_start(
                    out=out_2[:, 4 * Q : 4 * Q + 4, cols].rearrange("g r m -> r g m").bitcast(I32),
                    in_=y_s[32 * Q : 32 * Q + 4, :, cols].bitcast(I32),
                )

        nc.gpsimd.dma_start(out=c_col[:], in_=c.rearrange("(g p t) -> p g t", g=2, t=4))
        nc.gpsimd.dma_start(out=g_col[:], in_=g.rearrange("(g p t) -> p g t", g=2, t=4))
        nc.gpsimd.dma_start(out=s_row[:], in_=s.rearrange("(j p) -> j p", p=P))
        load_x(0, 0, 0, 2)
        load_w(0)
        load_scales(nc.sync, w_sraw, w_scales)
        load_x(0, 1, 0, 2)
        load_w(1)
        load_x(1, 0, 0, 2)
        load_x(1, 1, 0, 2)
        nc.sync.dma_start(out=a_raw[:].bitcast(I32), in_=a_in.bitcast(I32))
        load_scales(nc.sync, a_s, a_scales)
        with tc.manual_schedule():
            knots_g()
            turn_x(0, 0, 1)
            order_w(0)
            turn_x(0, 0, 0)
            copy_x(0, 0, 1, False)
            copy_x(0, 0, 0, False)
            quant_x(0, 0, 1, 0)
            quant_x(0, 0, 1, 1)
            order_w(1)
            knots_a()
            turn_x(0, 1, 1)
            turn_x(0, 1, 0)
            stage1(0, 0, 3, 0, 2)
            stage1(0, 0, 0, 0, 2)
            stage1(0, 0, 2, 0, 2)
            stage1(0, 0, 1, 0, 2)
            copy_x(0, 1, 0, False)
            squash(0, 0, 3, 0, 2)
            copy_x(0, 1, 1, False)
            squash(0, 0, 0, 0, 2)
            squash(0, 0, 2, 0, 2)
            squash(0, 0, 1, 0, 2)
            turn_x(1, 0, 1)
            turn_x(1, 0, 0)
            knots_t()
            turn_x(1, 1, 1)
            turn_x(1, 1, 0)
            gain(0, 0, 0, 2, False)
            knots_d()
            quant_x(0, 1, 1, 0)
            quant_x(0, 1, 1, 1)
            stage1(0, 1, 3, 0, 2)
            stage1(0, 1, 2, 0, 2)
            stage1(0, 1, 0, 0, 2)
            stage1(0, 1, 1, 0, 2)
            copy_x(1, 0, 1, False)
            copy_x(1, 0, 0, False)
            copy_x(1, 1, 1, False)
            copy_x(1, 1, 0, False)
            squash(0, 1, 3, 0, 2)
            squash(0, 1, 2, 0, 2)
            squash(0, 1, 0, 0, 2)
            squash(0, 1, 1, 0, 2)
            stage1(0, 0, 3, 1, 2)
            stage1(0, 1, 2, 1, 2)
            stage1(0, 0, 1, 1, 2)
            stage1(0, 0, 0, 1, 2)
            squash(0, 0, 3, 1, 2)
            knots_b()
            squash(0, 1, 2, 1, 2)
            squash(0, 0, 1, 1, 2)
            squash(0, 0, 0, 1, 2)
            stage1(0, 0, 2, 1, 2)
            stage1(0, 1, 3, 1, 2)
            stage1(0, 1, 1, 1, 2)
            stage1(0, 1, 0, 1, 2)
            squash(0, 0, 2, 1, 2)
            squash(0, 1, 3, 1, 2)
            squash(0, 1, 0, 1, 2)
            squash(0, 1, 1, 1, 2)
            quant_x(1, 0, 2, 1)
            quant_x(1, 0, 2, 0)
            gain(0, 1, 0, 2, False)
            gain(0, 0, 1, 2, False)
            knots_c()
            gain(0, 1, 1, 2, False)
            quant_z(0, 0)
            quant_z(0, 1)
            stage1(1, 0, 0, 0, 1)
            stage1(1, 1, 3, 0, 1)
            stage1(1, 0, 1, 0, 1)
            stage1(1, 0, 2, 0, 1)
            squash(1, 0, 0, 0, 1)
            squash(1, 1, 3, 0, 1)
            squash(1, 0, 1, 0, 1)
            squash(1, 0, 2, 0, 1)
            stage1(1, 0, 3, 0, 1)
            stage1(1, 1, 0, 0, 1)
            stage1(1, 1, 2, 0, 1)
            stage1(1, 1, 1, 0, 1)
            squash(1, 0, 3, 0, 1)
            squash(1, 1, 0, 0, 1)
            squash(1, 1, 2, 0, 1)
            scale_z(1, 1, 2)
            squash(1, 1, 1, 0, 1)
            scale_z(1, 1, 1)
            scale_z(1, 1, 0)
            scale_z(1, 1, 3)
            stage2(0, 0)
            stage2(3, 0)
            stage2(1, 0)
            stage2(2, 0)
            gain(1, 0, 0, 1, False)
            whole(0, 0)
            quant_z(1, 0)
            rest(0, 0)
            whole(1, 0)
            gain(1, 1, 0, 1, True)
            rest(1, 0)
            whole(2, 0)
            quant_z(1, 1)
            rest(2, 0)
            stage2(1, 1)
            stage2(2, 1)
            whole(3, 0)
            whole(1, 1)
            rest(1, 1)
            stage2(0, 1)
            stage2(3, 1)
            waves(0, 0, 2)
            waves(1, 0, 2)
            waves(2, 0, 2)
            waves(1, 1, 2)
            whole(0, 1)
            whole(2, 1)
            rest(0, 1)
            whole(3, 1)
            rest(3, 0)
            rest(3, 1)
            rest(2, 1)
            terms(1, 2, 1)
            stage2(6, 1)
            stage2(4, 0)
            stage2(4, 1)
            stage2(7, 0)
            turn_y(1, 1)
            turn_y(1, 0)
            waves(0, 1, 2)
            waves(3, 0, 1)
            waves(2, 1, 2)
            empty_y(1, 1, True)
            empty_y(1, 0, True)
            whole(4, 1)
            whole(4, 0)
            rest(4, 1)
            whole(6, 1)
            terms(0, 2, 1)
            whole(7, 0)
            rest(4, 0)
            terms(3, 1, 1)
            rest(6, 1)
            rest(7, 0)
            stage2(5, 0)
            stage2(5, 1)
            stage2(6, 0)
            turn_y(0, 1)
            turn_y(0, 0)
            turn_y(3, 0)
            turn_y(3, 1)
            waves(4, 0, 1)
            whole(5, 0)
            whole(5, 1)
            whole(6, 0)
            terms(2, 2, 1)
            lay_y(1, 0, 2)
            rest(6, 0)
            rest(5, 0)
            rest(5, 1)
            empty_y(0, 0, True)
            empty_y(0, 1, True)
            terms(4, 1, 1)
            lay_y(0, 0, 2)
            quant_y(1)
            empty_y(3, 0, True)
            empty_y(3, 1, False)
            waves(5, 0, 1)
            turn_y(4, 0)
            turn_y(4, 1)
            turn_y(2, 1)
            stage2(7, 1)
            turn_y(2, 0)
            empty_y(4, 0, False)
            lay_y(3, 0, 2)
            quant_y(0)
            empty_y(4, 1, False)
            empty_y(2, 1, True)
            quant_y(3)
            terms(5, 1, 1)
            whole(7, 1)
            lay_y(4, 0, 2)
            empty_y(2, 0, False)
            waves(6, 0, 1)
            rest(7, 1)
            lay_y(2, 0, 2)
            quant_y(4)
            quant_y(2)
            terms(6, 1, 1)
            turn_y(5, 0)
            turn_y(5, 1)
            turn_y(6, 1)
            turn_y(6, 0)
            empty_y(5, 0, True)
            waves(7, 0, 1)
            empty_y(5, 1, False)
            lay_y(5, 0, 2)
            empty_y(6, 1, False)
            quant_y(5)
            store_scales(0, 6)
            empty_y(6, 0, True)
            terms(7, 1, 2)
            turn_y(7, 0)
            turn_y(7, 1)
            lay_y(6, 0, 2)
            empty_y(7, 0, True)
            quant_y(6)
            empty_y(7, 1, False)
            lay_y(7, 0, 1)
            lay_y(7, 1, 1)
            quant_y(7)
            store_scales(6, 2)
